import numpy as np, ml_dtypes
CORES = [2,6,10,14,18,22,26,30]
N = 8
BF = ml_dtypes.bfloat16
def gentries(a):
    return np.ascontiguousarray(a.reshape(8, 16, -1).transpose(0, 2, 1)).reshape(8, -1)
def gtable(e):
    e = np.asarray(e); return np.ascontiguousarray(e.reshape(8, -1, 16).transpose(0, 2, 1)).reshape(128, -1).astype(np.int32)
L, B, V, W, DAYS, INTERVALS, H = 64, 32, 2048, 8192, 3, 2, 11
def parts(rng):
    x = rng.integers(28, 100, (N, 8, 1, V)) + rng.integers(-20, 21, (N, 8, 16, V))
    z = rng.integers(0, 65536, (N, 8, V))
    e = rng.integers(-75, 46, (8, 1, W)) + rng.integers(-20, 21, (8, 16, W))
    return x, z, e
def pack(x, z, e):
    x = np.minimum(np.maximum(x, 0), 127).reshape(N, 128, V); e = np.minimum(np.maximum(e, -128), 128).reshape(1, 128, W)
    return {"x": x.astype(np.float32).astype(BF), "boat": np.stack([gtable(a) for a in z]), "enc": np.repeat(e, N, axis=0).astype(np.float32).astype(BF)}
def timed(rng, z, g):
    r = rng.integers(0, W); z[:, g] = r + W * rng.integers(0, 65536 // W, (N, V))
    return (138 * r + 811 * np.arange(DAYS * INTERVALS + DAYS)) % W
def setup_inputs(rng):
    return pack(*parts(rng))
def setup_inputs_ties(rng):
    x, z, e = parts(rng)
    x = rng.integers(20, 100, (1, 8, 16, 1)) + rng.integers(0, 2, (N, 8, 1, V))
    n = rng.choice(np.array([0, H - 1, H - 1, H, H, H + 1, 16]), (8, 1, W)); up = np.argsort(rng.random((8, 16, W)), axis=1) < n
    e = rng.choice(np.array([0, 0, 1, 1, 1, 2]), (8, 1, W)) - 1 + up
    return pack(x, z, e)
def setup_inputs_order(rng):
    x, z, e = parts(rng); b = np.arange(B); k = INTERVALS; q = b % (2 * k)
    st = np.stack([127 - 2 * b, 1 + 2 * b, np.where(q < k, 10 * (k - q), 10 * (3 * k - q)), 64 + 0 * b, np.where(b == 0, 120, np.where(b == B - 1, 127, 1 + 2 * b))])
    kind = rng.integers(0, 6, (N, 8, L)); kind[:, :, :6] = np.arange(6); kind[:, :, L - 6:] = rng.permutation(6)
    s = st[np.minimum(kind, 4)].transpose(0, 1, 3, 2).reshape(N, 8, 1, V)
    x = np.where(np.tile(kind == 5, (1, 1, B))[:, :, None, :], x, s)
    e = np.where(rng.random((8, 16, W)) < rng.random((8, 1, W)), 1, rng.integers(-1, 1, (8, 16, W)))
    return pack(x, z, e)
def setup_inputs_alike(rng):
    x, z, e = parts(rng); zz = z.reshape(N, 8, B, L).copy(); inv = pow(37, -1, W)
    for b in range(1, B):
        c = rng.choice(np.array([0, W - 1]), (N, 8, L))
        zz[:, :, b] = (c - 101 * zz[:, :, b - 1]) % W * inv % W + W * rng.integers(0, 65536 // W, (N, 8, L))
    zz[:, :, :, 1::2] = rng.choice(np.array([0, 65535, 65535, 1]), (N, 8, B, len(range(1, L, 2))))
    e[:, :, 0] = rng.integers(-10, 31, (8, 16)); e[:, :, W - 1] = rng.integers(-30, 11, (8, 16))
    g = rng.permutation(8); odd = np.arange(N)[:, None, None] % 2 == 1
    for i, (c, s) in enumerate(((0, 1), (W - 1, -1))):
        a = rng.integers(0, W, L); b = (c - 811 * DAYS * INTERVALS - 101 * a) % W * inv % W
        zz[:, g[i]] = np.where(odd, b, a) + W * rng.integers(0, 65536 // W, (N, B, L))
        e[g[i]][:, c] = s * rng.integers(112, 129, 16); e[g[i]][:, c + s] = -s * rng.integers(112, 129, 16)
    return pack(x, zz.reshape(N, 8, V), e)
def setup_inputs_flat(rng):
    x, z, e = parts(rng); g = rng.permutation(8); k = INTERVALS; last = (DAYS - 1) * k
    e[g[0]] = -128; e[g[1]] = 128
    x[:, g[1]] = np.where(rng.random((N, 1, V)) < 0.5, x[:, g[1]], 127 * rng.integers(0, 2, (N, 1, V)))
    e[g[2]] = 127; x[:, g[2]] = 127 * rng.integers(0, 2, (N, 16, V))
    e[g[3]] = rng.choice(np.array([-127, -126]), (1, W)); x[:, g[3]] = 127 * rng.integers(0, 2, (N, 1, V))
    c = timed(rng, z, g[4]); e[g[4]][:, c[:k - 1]] = -128; e[g[4]][:, c[k - 1]] = 128
    c = timed(rng, z, g[5]); e[g[5]][:, c[last]] = -128; e[g[5]][:, c[last + 1]] = rng.integers(127, 129, 16)
    c = timed(rng, z, g[6]); e[g[6]][:, c[:-1]] = -128; e[g[6]][:, c[[last, last + k - 1]]] = 0
    b = np.arange(B)[:, None]; s = np.where(b == 0, 120, np.where(b == B - 1, 127, 1 + 2 * b))
    x[:, g[6]] = np.where(rng.random((N, 1, 1, L)) < 0.5, s, x[:, g[6]].reshape(N, 16, B, L)).reshape(N, 16, V)
    return pack(x, z, e)
def setup_inputs_spread(rng):
    x = np.floor(127.99 * np.exp2(-6 * rng.random((N, 8, 1, V))) * rng.random((N, 8, 16, V))).astype(np.int64)
    z = np.minimum(np.exp2(16 * rng.random((N, 8, V))).astype(np.int64), 65535) - 1 + rng.integers(0, 2, (N, 8, V))
    e = np.rint(128 * np.exp2(-7 * rng.random((8, 1, W))) * (0.25 + 0.75 * rng.random((8, 16, W)))).astype(np.int64) * (2 * rng.integers(0, 2, (8, 1, W)) - 1)
    return pack(x, z, e)
def check_inputs(d):
    bad = []
    for k, lo, hi in (("x", 0, 127), ("boat", 0, 65535), ("enc", -128, 128)):
        v = np.asarray(d[k]).astype(np.float32)
        if not np.all((v >= lo) & (v <= hi) & (v == np.floor(v))): bad.append("range of " + k)
    v = np.asarray(d["enc"]).astype(np.float32)
    if not np.all(v == v[:1]): bad.append("enc alike on all ranks")
    return bad
def beats(xi, zi, xj, zj, e, t):
    c = (37 * zi + 101 * zj + 811 * t) & (W - 1)
    v = np.take_along_axis(e, c[:, :, None, :], 3)
    return np.add.reduce((xi + v > xj).astype(np.int64), axis=2) >= H
def reference(x, boat, enc):
    X = x.astype(np.float32).reshape(N, 8, 16, V); E = enc.astype(np.float32).reshape(N, 8, 16, W)
    Z = np.stack([gentries(a) for a in boat]).astype(np.int64)
    for day in range(DAYS):
        rowing = np.ones((N, 8, V), bool); place = np.tile(np.arange(V), (N, 8, 1))
        for k in range(INTERVALS):
            row = rowing.reshape(N, 8, B, L); rival = np.full((N, 8, B, L), -1); last = np.full((N, 8, L), -1)
            for b in range(B):
                rival[:, :, b] = np.where(row[:, :, b], last, -1)
                last = np.where(row[:, :, b], b * L + np.arange(L), last)
            rival = rival.reshape(N, 8, V); j = np.maximum(rival, 0)
            w = beats(X, Z, np.take_along_axis(X, j[:, :, None, :], 3), np.take_along_axis(Z, j, 2), E, day * INTERVALS + k) & (rival >= 0)
            w = w.reshape(N, 8, B, L); bump = np.zeros((N, 8, B, L), bool); before = np.zeros((N, 8, L), bool)
            for b in range(B):
                bump[:, :, b] = w[:, :, b] & ~before
                before = np.where(row[:, :, b], bump[:, :, b], before)
            i0, i1, i2 = np.nonzero(bump.reshape(N, 8, V)); jj = j[i0, i1, i2]
            place[i0, i1, i2] = jj; place[i0, i1, jj] = i2
            rowing[i0, i1, i2] = False; rowing[i0, i1, jj] = False
        X = np.take_along_axis(X, place[:, :, None, :], 3); Z = np.take_along_axis(Z, place, 2)
        hx, hz = np.array(X[1:, :, :, :L]), np.array(Z[1:, :, :L]); fx, fz = np.array(X[:-1, :, :, V - L:]), np.array(Z[:-1, :, V - L:])
        w = beats(hx, hz, fx, fz, E[1:], DAYS * INTERVALS + day); wx = w[:, :, None, :]
        X[1:, :, :, :L] = np.where(wx, fx, hx); Z[1:, :, :L] = np.where(w, fz, hz)
        X[:-1, :, :, V - L:] = np.where(wx, hx, fx); Z[:-1, :, V - L:] = np.where(w, hz, fz)
    return {"yx": X.reshape(N, 128, V).astype(BF), "yb": np.stack([gtable(a) for a in Z]).astype(np.float32)}

@@ -1,0 +1,572 @@
+import numpy as np
+from concourse.bass import DstId, RemoteDMATransfer
+from concourse.mybir import AluOpType as A, AxisListType, ActivationFunctionType as F
+
+BIG = float(2 ** 25)
+ZN = 96
+TW = ZN + 2048
+DAYS = 3
+SEG_FIRST = [(0, 24, "S"), (24, 44, "V"), (44, 64, "V"), (64, 88, "S"), (88, 108, "V"), (108, 128, "V")]
+SEG0 = [(0, 22, "M"), (22, 48, "M"), (48, 64, "M"), (64, 88, "M"), (88, 106, "S"), (106, 128, "S")]
+SEG1 = [(0, 26, "S"), (26, 46, "V"), (46, 64, "V"), (64, 90, "S"), (90, 116, "S"), (116, 128, "V")]
+FIN = [(4, 34, "s"), (34, 64, "v"), (64, 94, "s"), (94, 124, "v")]
+TRIES = 6000
+NE = 8
+
+SCRATCH = {}
+for dt_, bufs_ in (
+        ("bfloat16", dict(E=8192, X=2048, T0=TW, T1=TW, T2=TW, D=2048, G1=2048, G2=2048, C=2048, XO=2048, XE=128, Ds=256,
+                          Cs=256, W=144, Id=128, nId=128, bF=128, b0=128, b1=128, bs=16, bd=128, neg=128, tau=136, n=128,
+                          sgn=128, nr=128, zt=128, Lc=136, cst=128)),
+        ("float32", dict(MB0=400, MB1=400, MB2=400, ZO=128, val=132, vB=128, LB=132, vr=128, df=128, d0=132, vm=128, e=128,
+                         tm=128, fp=16, own=16, m6=16, mw=16, ix=32, iq=144, iI=128, col=8, rw=64, rm=64, mk=16,
+                         mu=16, inv=16, ka=48, oz=16, oc=16, i5=16)),
+        ("int32", dict(Bt=128, vi=128, p16=128, zz=128, B=132, Bm=128, ci=128, cj=128, sm=16, sn=16, fz=16, m7=16, m8=16,
+                       m9=16, ixi=32, ik=4, i1=128, i2=128, i3=128, i4=16)),
+        ("uint16", dict(oc0=128, oc1=128, op=128, orv=128, oE=16, om=16, of=16, sP=8, sQ=8, sE=2, sZ=2, sD=16))):
+    for name_, n_ in bufs_.items():
+        SCRATCH[name_] = ("sbuf", [128, n_], dt_)
+for name_ in ("pb0", "pb1", "pb2", "py0", "py1", "ps", "pv", "pw"):
+    SCRATCH[name_] = ("psum", [128, 512], "float32")
+SEMAPHORES = ["qv", "qs", "qt", "qg", "ls", "ar0", "ar1", "ar2"] + ["dm%d" % i for i in range(12)]
+
+GUESS = [(0.00104, 0.00162, 0.0006, 0.08, 3.0, 1.5, 0.003), (0.00088, 0.0011, 0.00045, 0.06, 2.5, 1.0, 0.0025),
+         (0.0012, 0.0021, 0.0006, 0.1, 3.5, 2.5, 0.004), (0.00104, 0.0014, 0.001, 0.08, 4.0, 1.5, 0.003)]
+ORDER = {}
+
+
+def R(b, lo, hi, st=1):
+    return (b, lo, hi, st)
+
+
+def build(T, rank, n_ranks, topo, core):
+    ops = []
+
+    def ap(r):
+        if len(r) == 2:
+            return ap(r[0]).indirect(ap(r[1]))
+        b, lo, hi, st = r
+        if st < 0:
+            return T[b][:, hi - 1:(lo - 1 if lo > 0 else None):st]
+        return T[b][:, lo:hi] if st == 1 else T[b][:, lo:hi:st]
+
+    def flat(rs):
+        out = []
+        for r in rs:
+            if isinstance(r, tuple):
+                out += list(r) if len(r) == 2 else [r]
+        return out
+
+    def n_of(r):
+        return 16 * n_of(r[1]) if len(r) == 2 else len(range(r[1], r[2], abs(r[3])))
+
+    def two(rs):
+        return all(SCRATCH[r[0]][2] in ("bfloat16", "uint16") for r in rs)
+
+    def sc(s):
+        return ap(s) if isinstance(s, tuple) else s
+
+    def add(q, fn, rd, wr, t, kind="c"):
+        ops.append([q, fn, flat(rd), flat(wr), t, kind])
+
+    def vt(o, i, k, fix=0.05):
+        return (fix, n_of(i), 1) if len(i) == 2 else (fix, max(64, n_of(o) * k), 0)
+
+    def tt(o, a, b, op):
+        k = 1 if len(a) == 2 or "psum" in (SCRATCH[a[0]][0], SCRATCH[b[0]][0]) else 2
+        add("v", lambda g: g.vector.tensor_tensor(ap(o), ap(a), ap(b), op), [a, b], [o], vt(o, a, k))
+
+    def ts(o, a, s1, s2, op0, op1=None):
+        k = 0.5 if len(a) == 4 and two([o, a]) else 1
+        if op1 is None:
+            add("v", lambda g: g.vector.tensor_scalar(ap(o), ap(a), sc(s1), None, op0), [a, s1], [o], vt(o, a, k))
+        else:
+            add("v", lambda g: g.vector.tensor_scalar(ap(o), ap(a), sc(s1), sc(s2), op0, op1), [a, s1, s2], [o], vt(o, a, k))
+
+    def cp(o, a):
+        add("v", lambda g: g.vector.tensor_copy(ap(o), ap(a)), [a], [o], vt(o, a, 1))
+
+    def ms(o, c):
+        add("v", lambda g: g.vector.memset(ap(o), c), [], [o], vt(o, o, 0.5 if two([o]) else 1))
+
+    def scan(o, a, b, init, op0, op1):
+        add("v", lambda g: g.vector.tensor_tensor_scan(ap(o), ap(a), ap(b), init, op0, op1), [a, b], [o],
+            vt(o, a, 0.5 if two([o, a, b]) else 1))
+
+    def act(o, a, f, **kw):
+        add("s", lambda g: g.scalar.activation(ap(o), ap(a), f, **kw), [a], [o], vt(o, a, 1, 0.065))
+
+    def mms(items, start=True, stop=True):
+        for k, run in enumerate(items):
+            def fn(g, run=run, first=start and k == 0, end=stop and k == len(items) - 1):
+                for m, (o, l, r) in enumerate(run):
+                    ins = g.tensor.matmul(ap(o), ap(l), ap(r), first and m == 0, end and m == len(run) - 1)
+                return ins
+            add("t", fn, [x for o, l, r in run for x in (l, r)], [run[0][0]],
+                (0.0, sum(max(64, n_of(r)) for o, l, r in run), 2))
+
+    def iota(o, pat, base, ch=0):
+        kw = {} if SCRATCH[o[0]][2] == "int32" else {"allow_small_or_imprecise_dtypes": True}
+        add("g", lambda g: g.iota(ap(o), pat, base, ch, **kw), [], [o], (0.13, 2 * n_of(o), 0))
+
+    def dma(q, o, a, rd, wr, kib):
+        add(q, (lambda g: g.sync.dma_start(o, a)) if q == "y" else (lambda g: g.scalar.dma_start(o, a)), rd, wr,
+            (2.0, kib, 6), "dma")
+
+    bank = [0]
+
+    def pb(n):
+        bank[0] = (bank[0] + 1) % 3
+        return R("pb%d" % bank[0], 0, n)
+
+    def L(b, lo=0):
+        return R(b, lo, lo + 128)
+
+    def wide(b, c0, c1, off=0):
+        return R(b, off + 16 * c0, off + 16 * c1)
+
+    def py(h):
+        return R("py%d" % (h // 64), 0, 64)
+
+    P = R("col", 0, 1)
+    Ew = R("E", 0, 8192)
+    Id, nId = L("Id"), L("nId")
+    PA, PCS, PSB = L("pv"), L("pv", 128), L("pv", 256)
+
+    for d in range(DAYS):
+        if rank == 0:
+            ms(R("MB%d" % d, 68, 136), 512.0)
+        if rank == n_ranks - 1:
+            ms(R("MB%d" % d, 0, 68), 512.0)
+    extra = len(ops)
+    dma("y", T.Bt[:, :], T.boat[:, :], [], [L("Bt")], 64)
+    dma("y", T.X[:, :], T.x[:, :], [], [R("X", 0, 2048)], 576)
+    dma("y", T.E[:, :], T.enc[:, :], [], [Ew], 2624)
+
+    iota(R("ik", 0, 1), [[0, 1]], 0, 1)
+    iota(R("i4", 0, 8), [[1, 4], [64, 2]], 0)
+    iota(L("i1"), [[16, 4], [64, 32]], 0)
+    iota(L("iI"), [[1, 128]], 0, -1)
+    iota(R("iq", 0, 144), [[1, 144]], -15)
+    iota(L("i2"), [[1, 128]], 6)
+    iota(L("i3"), [[0, 4], [8192, 32]], 811)
+    iota(R("rw", 0, 8), [[-1, 2], [32, 4]], 31)
+    iota(R("rw", 8, 16), [[-1, 2], [32, 4]], 1)
+    iota(R("rw", 16, 32), [[1, 4], [32, 4]], 0)
+    iota(R("rw", 32, 48), [[4, 2], [0, 2], [1, 4]], 64)
+    iota(R("i4", 8, 16), [[4, 8]], 0)
+    iota(R("i5", 0, 16), [[72, 2], [0, 2], [16, 4]], 0)
+    iota(R("ixi", 0, 16), [[16, 4], [4, 4]], 35)
+    iota(R("ixi", 16, 32), [[18, 2], [0, 2], [4, 4]], 0)
+    ts(R("ik", 1, 2), R("ik", 0, 1), 15, None, A.bitwise_and)
+    ts(R("ik", 2, 3), R("ik", 0, 1), 112, None, A.bitwise_and)
+    cp(R("col", 0, 2), R("ik", 1, 3))
+    ts(R("col", 2, 3), P, 4.0, None, A.mult)
+    ts(R("sP", 0, 8), R("i4", 0, 8), R("col", 2, 3), None, A.add)
+    ts(L("op"), L("i1"), P, None, A.add)
+    ts(Id, L("iI"), 0.0, None, A.is_equal)
+    ts(nId, L("iI"), 0.0, -1.0, A.is_equal, A.mult)
+    ts(R("W", 0, 144), R("iq", 0, 144), R("col", 1, 2), -BIG, A.is_equal, A.mult)
+    ts(R("i2", 0, 128, 32), R("i2", 0, 128, 32), 26.0, 1.0 / 32, A.add, A.mult)
+    ts(PCS, L("i2"), 65536.0, None, A.mult)
+    cp(L("cst"), L("i2"))
+    ms(R("cst", 31, 128, 32), 0.0)
+    cp(PSB, L("i3"))
+    ts(R("mk", 0, 16), R("iq", 15, 31), P, None, A.is_equal)
+    for k in range(3):
+        tt(R("rm", 16 * k, 16 * k + 16), R("rw", 16 * k, 16 * k + 16), R("mk", 0, 16), A.mult)
+        add("v", lambda g, k=k: g.vector.tensor_reduce(T.col[:, 3 + k:4 + k], T.rm[:, 16 * k:16 * k + 16], AxisListType.X, A.add),
+            [R("rm", 16 * k, 16 * k + 16)], [R("col", 3 + k, 4 + k)], (0.05, 64, 0))
+    cp(R("sE", 0, 1), R("col", 3, 4))
+    ts(R("sQ", 0, 8), R("i4", 8, 16), R("col", 4, 5), None, A.add)
+    cp(R("sZ", 0, 1), R("col", 5, 6))
+    ts(R("sD", 0, 16), R("i5", 0, 16), P, None, A.add)
+    ts(R("ix", 0, 32), R("ixi", 0, 32), 65536.0, None, A.mult)
+    for name, segs, heads in (("bF", SEG_FIRST, True), ("b0", SEG0, True), ("b1", SEG1, False)):
+        ms(L(name), 10.5 * BIG)
+        runs = []
+        for c0, c1, rt in segs:
+            if rt == "S":
+                if runs and runs[-1][1] == c0:
+                    runs[-1][1] = c1
+                else:
+                    runs.append([c0, c1])
+        for c0, c1 in runs:
+            ms(R(name, c0, c1), 5.0 * BIG)
+        if heads:
+            ms(R(name, 0, 128, 32), 64.0 * BIG)
+    ms(R("bs", 0, 16), 10.5 * BIG)
+    ms(L("neg"), -1.0)
+    ms(L("zt"), 0.0)
+    ms(R("tau", 128, 136), BIG)
+    ms(R("Lc", 0, 1), 0.0)
+    ms(R("val", 0, 132, 129), 0.0)
+    ms(R("LB", 0, 1), 0.0)
+    ms(R("d0", 128, 129), 0.0)
+    ms(R("B", 0, 1), 0)
+    ms(R("pw", 0, 1), 0.0)
+    ms(R("pw", 336, 409, 72), 0.0)
+    for d in range(DAYS):
+        ms(R("T%d" % d, 0, ZN), 512.0)
+        if d < DAYS - 1:
+            ms(R("ka", 16 * d, 16 * d + 16), float(811 * (2 * DAYS + d)))
+            ms(R("ka", 16 * d + 4, 16 * d + 12), float(811 * (2 * d + 2)))
+    ms(R("mu", 0, 8), 101.0)
+    ms(R("mu", 8, 16), 37.0)
+    ms(R("inv", 0, 8), 1.0 / 37)
+    ms(R("inv", 8, 16), 1.0 / 101)
+
+    def reduce(y, bias, cb, c0, c1, dyn=None, stop=True):
+        mms([[(y, Id, bias)] + ([(y, nId, dyn)] if dyn else [])
+             + [(y, R("W", 15 - p, 143 - p), R(cb, 16 * c0 + p, 16 * c1, 16)) for p in range(16)]], True, stop)
+
+    def numbers(t, h, w):
+        ts(R("pv", h, h + w), R("zz", h, h + w), 37.0, float(811 * t), A.mult, A.add)
+        ts(R("B", h + 1, h + w + 1), R("zz", h, h + w), 101.0, None, A.mult)
+        tt(R("ci", h, h + w), R("pv", h, h + w), R("B", h, h + w), A.add)
+        ts(R("cj", h, h + w), R("ci", h, h + w), 8191, None, A.bitwise_and)
+        cp(R("oc0", h, h + w), R("cj", h, h + w))
+
+    def values():
+        tt(L("val", 1), L("zz"), PCS, A.add)
+        ts(L("Bm"), L("B", 1), 8191, None, A.bitwise_and)
+        tt(L("vB"), L("Bm"), PSB, A.add)
+
+    def halves(done, bias, dyn=None, stop=True):
+        if done in (64, 128):
+            h = done - 64
+            reduce(py(h), R(bias, h, done), "C", h, done, dyn and R(dyn, h, done), stop)
+
+    def race(rt, c0, c1, eg, xs, xq):
+        q = pb(16 * (c1 - c0))
+        if rt == "M":
+            mms([[(q, Id, xq), (q, nId, xs)]])
+            act(wide("D", c0, c1), q, F.Copy)
+            tt(wide("C", c0, c1), eg, wide("D", c0, c1), A.is_gt)
+        else:
+            act(wide("G1", c0, c1), eg, F.Copy)
+            mms([[(q, nId, xq), (q, Id, xs)], [(q, Id, wide("G1", c0, c1))]])
+            act(wide("C", c0, c1), q, F.Sign, bias=-0.5)
+
+    cp(L("zz"), (L("Bt"), R("sP", 0, 8)))
+    numbers(0, 0, 128)
+    values()
+    act(R("T0", 16, 80), R("X", 0, 64), F.Copy)
+    for c0 in range(0, 128, 32):
+        act(wide("T0", c0, c0 + 32, ZN), (R("X", 0, 2048), R("op", c0, c0 + 32)), F.Copy)
+        q = pb(512)
+        mms([[(q, Id, wide("T0", c0 - 1, c0 + 31, ZN)), (q, nId, wide("T0", c0, c0 + 32, ZN))]])
+        act(wide("D", c0, c0 + 32), q, F.Copy)
+    for c0, c1, rt in SEG_FIRST:
+        eg = (Ew, R("oc0", c0, c1))
+        if rt == "V":
+            tt(wide("C", c0, c1), eg, wide("D", c0, c1), A.is_gt)
+        else:
+            act(wide("G1", c0, c1), eg, F.Copy)
+            q = pb(16 * (c1 - c0))
+            mms([[(q, nId, wide("D", c0, c1))], [(q, Id, wide("G1", c0, c1))]])
+            act(wide("C", c0, c1), q, F.Sign, bias=-0.5)
+        halves(c1, "bF")
+
+    for d in range(DAYS):
+        Tn, Tx, MB, last = "T%d" % d, "T%d" % (d + 1), "MB%d" % d, d == DAYS - 1
+        Tw = R(Tn, 0, TW)
+        for h in (0, 64):
+            scan(R("tau", h, h + 64), R("neg", 0, 64), py(h), 1.0, A.mult, A.max)
+        tt(L("n"), L("tau"), L("tau", 1), A.min)
+        scan(L("Lc", 1), L("n"), L("cst"), 0.0, A.max, A.min)
+        ts(L("orv"), L("Lc"), 16.0, P, A.mult, A.add)
+        scan(L("LB", 1), L("n"), L("vB"), 0.0, A.max, A.min)
+        tt(L("ci"), PA, L("LB"), A.add)
+        ts(L("cj"), L("ci"), 8191, None, A.bitwise_and)
+        cp(L("oc1"), L("cj"))
+        act(L("sgn"), L("n"), F.Sign, scale=-1.0)
+        act(L("bd"), L("n"), F.Relu, scale=-128.0)
+        act(L("nr"), L("sgn"), F.Relu)
+        for c0, c1, rt in SEG1:
+            eg, xr, xs = (Ew, R("oc1", c0, c1)), (Tw, R("orv", c0, c1)), wide(Tn, c0, c1, ZN)
+            if rt == "V":
+                tt(wide("D", c0, c1), eg, xs, A.add)
+                tt(wide("C", c0, c1), xr, wide("D", c0, c1), A.is_lt)
+            else:
+                act(wide("G2", c0, c1), xr, F.Copy)
+                race(rt, c0, c1, eg, xs, wide("G2", c0, c1))
+            halves(c1, "b1", "bd")
+        scan(L("pw", 1), L("n"), L("val", 1), 0.0, A.max, A.min)
+        tt(L("vr"), L("val", 1), L("n"), A.min)
+        tt(L("df"), L("pw"), L("vr"), A.subtract)
+        tt(L("pw", 136), L("val"), L("tau"), A.max)
+        tt(L("pv", 384), L("pw", 136), L("val", 1), A.min)
+        tt(L("d0"), L("pv", 384), L("val", 1), A.subtract)
+        tt(L("vm"), L("pv", 384), L("d0", 1), A.subtract)
+        for h in (0, 64):
+            def H(b, lo=0, st=1):
+                return R(b, lo + h, lo + h + 64, st)
+            s0 = 272 + h // 8
+            scan(H("pw", 136), H("sgn"), py(h), BIG, A.mult, A.max)
+            tt(H("e"), H("pw", 136), H("df"), A.max)
+            scan(H("pw", s0, -1), H("nr", 0, -1), H("e", 0, -1), 0.0, A.mult, A.min)
+            tt(H("tm"), H("pw", s0), H("vm"), A.add)
+            tt(H("vi"), H("tm"), H("pw", s0 + 1), A.subtract)
+            ts(H("p16"), H("vi"), 12, 0xFF0, A.arith_shift_right, A.bitwise_and)
+            ts(H("zz"), H("vi"), 65535, None, A.bitwise_and)
+            if not last:
+                ts(H("op"), H("p16"), P, None, A.add)
+                numbers(2 * d + 2, h, 64)
+        ts(R("oE", 0, 16), (L("p16"), R("sE", 0, 1)), P, None, A.add)
+        ts(R(MB, 136, 140), R("zz", 31, 128, 32), 101.0, None, A.mult)
+        oh = 204 if last else 332
+        ts(R(MB, oh + 64, oh + 68), R("zz", 0, 128, 32), 37.0, None, A.mult)
+        act(R(MB, 140, 204), (Tw, R("oE", 0, 4)), F.Copy)
+        act(R(MB, oh, oh + 64), (Tw, R("oE", 12, 16)), F.Copy, scale=-1.0)
+        sends = []
+        if rank > 0:
+            sends.append((T.cores[rank - 1], oh, 0))
+        if rank < n_ranks - 1:
+            sends.append((T.cores[rank + 1], 136, 68))
+        sends.sort(key=lambda s: len(topo.engines(core, s[0])))
+        used, trs = [], []
+        for dst, so, do in sends:
+            en = [x for x in topo.engines(core, dst) if x not in used][:NE]
+            used += en
+            rid, pid, _ = topo.addr(dst)
+            trs.append(RemoteDMATransfer(dst_ids=[DstId(rid=rid, pnc=pid)], dma_engine_mask=sum(1 << x for x in en),
+                                         remote_sem=T.sem["ar%d" % d], src=T[MB][:, so:so + 68], dst=T[MB][:, do:do + 68]))
+        wr = ([R(MB, 68, 136)] if rank > 0 else []) + ([R(MB, 0, 68)] if rank < n_ranks - 1 else [])
+        add("g", lambda g, trs=trs: g.remote_dma_fused(trs, local_sem=T.sem.ls), [R(MB, 136, 204), R(MB, oh, oh + 68)], wr,
+            (0.0, 1, 4 if d else 7), ("rem", d, len(used)))
+        if not last:
+            act(R(MB, 204, 268), (Tw, R("oE", 4, 8)), F.Copy)
+            act(R(MB, 268, 332), (Tw, R("oE", 8, 12)), F.Copy, scale=-1.0)
+            tt(R("own", 0, 16), (L("zz"), R("sE", 0, 1)), R("ix", 0, 16), A.add)
+            tt(R("oz", 0, 16), (L("zz"), R("sE", 0, 1)), R("mu", 0, 16), A.mult)
+            tt(R("oc", 0, 16), R("oz", 0, 16), R("ka", 16 * d, 16 * d + 16), A.add)
+            for c0, c1, rt in SEG0:
+                xs = wide(Tx, c0, c1, ZN)
+                act(xs, (Tw, R("op", c0, c1)), F.Copy)
+                race(rt, c0, c1, (Ew, R("oc0", c0, c1)), xs, wide(Tx, c0 - 1, c1 - 1, ZN))
+                halves(c1, "b0", None, False)
+        else:
+            k = float(811 * (2 * DAYS + d))
+            ts(R("oc", 4, 8), R(MB, 136, 140), k, None, A.add)
+            ts(R("oc", 8, 12), R(MB, 268, 272), k, None, A.add)
+            tt(R("own", 4, 8), R("zz", 31, 128, 32), R("ix", 0, 4), A.add)
+            tt(R("own", 8, 12), R("zz", 0, 128, 32), R("ix", 4, 8), A.add)
+            ts(L("op"), (L("p16"), R("sQ", 0, 8)), P, None, A.add)
+            for c0, c1, q in FIN:
+                src = (Tw, R("op", c0, c1))
+                if q == "s":
+                    act(wide("XO", c0, c1), src, F.Copy)
+                else:
+                    cp(wide("XO", c0, c1), src)
+            dma("y", T.yx[:, 64:1024], T.XO[:, 64:1024], [R("XO", 64, 1024)], [], 256)
+            dma("y", T.yx[:, 1024:1984], T.XO[:, 1024:1984], [R("XO", 1024, 1984)], [], 256)
+            cp(L("ZO"), (L("zz"), R("sQ", 0, 8)))
+        fz = (R(MB, 0, 136), R("sZ", 0, 1))
+        tt(R("sm", 0, 16), fz, R("oc", 0, 16), A.add)
+        a, b = (4, 12) if last else (0, 16)
+        ts(R("sn", a, b), R("sm", a, b), 8191, None, A.bitwise_and)
+        cp(R("om", a, b), R("sn", a, b))
+        tt(wide("Ds", a, b), (R(MB, 0, 136), R("sD", a, b)), R(MB, 140, 140 + 16 * (b - a)), A.add)
+        tt(wide("Cs", a, b), (Ew, R("om", a, b)), wide("Ds", a, b), A.is_gt)
+        reduce(R("ps", a, b), R("bs", a, b), "Cs", a, b)
+        tt(R("fz", 0, 16), fz, R("inv", 0, 16), A.mult)
+        tt(R("fp", 0, 16), R("fz", 0, 16), R("ix", 16, 32), A.add)
+        tt(R("m6", a, b), R("ps", a, b), R("fp", a, b), A.max)
+        tt(R("m7", a, b), R("m6", a, b), R("own", a, b), A.min)
+        ts(R("m8", a, b), R("m7", a, b), 14, 0x1FC, A.arith_shift_right, A.bitwise_and)
+        if not last:
+            ts(R("mw", 0, 16), R("ps", 0, 16), 0.0, 128.0, A.is_lt, A.mult)
+            tt(R("zt", 31, 128, 32), R("ps", 4, 8), R("mw", 0, 4), A.mult)
+            tt(R("zt", 1, 128, 32), R("ps", 8, 12), R("mw", 12, 16), A.mult)
+            for h in (0, 64):
+                mms([[(py(h), Id, R("zt", h, h + 64))]], False, True)
+            ts(R("of", 0, 8, 2), R("m8", 0, 4), P, None, A.add)
+            ts(R("of", 12, 16), R("m8", 12, 16), P, None, A.add)
+            act(R(Tx, 16, 80), (R(MB, 0, 400), R("of", 12, 16)), F.Abs)
+            for lq in range(4):
+                act(wide(Tx, 32 * lq + 31, 32 * lq + 32, ZN), (R(MB, 0, 400), R("of", 2 * lq, 2 * lq + 1)), F.Abs)
+            ts(R("zz", 31, 128, 32), R("m7", 0, 4), 65535, None, A.bitwise_and)
+            ts(R("zz", 0, 128, 32), R("m7", 12, 16), 65535, None, A.bitwise_and)
+            ts(R("B", 1, 129, 32), R("zz", 0, 128, 32), 101.0, None, A.mult)
+            ts(R("pv", 31, 128, 32), R("zz", 31, 128, 32), 37.0, float(811 * (2 * d + 2)), A.mult, A.add)
+            values()
+        else:
+            ts(R("of", 4, 12), R("m8", 4, 12), P, None, A.add)
+            act(L("XE"), (R(MB, 0, 272), R("of", 4, 12)), F.Abs)
+            dma("s", T.yx[:, 0:64], T.XE[:, 64:128], [R("XE", 64, 128)], [], 16)
+            dma("y", T.yx[:, 1984:2048], T.XE[:, 0:64], [R("XE", 0, 64)], [], 16)
+            ts(R("m9", 4, 12), R("m7", 4, 12), 65535, None, A.bitwise_and)
+            cp(R("ZO", 124, 128), R("m9", 4, 8))
+            cp(R("ZO", 0, 4), R("m9", 8, 12))
+            dma("y", T.yb[:, :], T.ZO[:, :], [L("ZO")], [], 64)
+    return ops, extra
+
+
+def meets(a, b):
+    if a[2] <= b[1] or b[2] <= a[1]:
+        return False
+    sa, sb = abs(a[3]), abs(b[3])
+    return not (sa == sb and sa > 1 and (a[1] - b[1]) % sa)
+
+
+def depend(ops):
+    deps, hist = [], {}
+    for i, (q, _, rd, wr, _, _) in enumerate(ops):
+        dp = set()
+        acc = [(r, False) for r in rd] + [(r, True) for r in wr]
+        for r, w in acc:
+            psum = SCRATCH[r[0]][0] == "psum"
+            for j, r2, w2 in hist.get(r[0], []):
+                if ((w or w2) and meets(r, r2)) or (psum and (ops[j][0] != q or q == "t")):
+                    dp.add(j)
+        for r, w in acc:
+            hist.setdefault(r[0], []).append((i, r, w))
+        deps.append(dp)
+    anc = []
+    for i, dp in enumerate(deps):
+        far = 0
+        for j in dp:
+            far |= anc[j]
+        deps[i] = sorted(j for j in dp if not far >> j & 1)
+        for j in dp:
+            far |= 1 << j
+        anc.append(far if ops[i][5] in ("c", "dma") else 0)
+    return deps
+
+
+def times(ops, gs):
+    gs = list(gs) + [gs[4] + gs[5]]
+    return [o[4][0] + o[4][1] * gs[o[4][2]] for o in ops]
+
+
+def span(ops, deps, seq, gs):
+    t, free, end = times(ops, gs), {}, {}
+    for i in seq:
+        q = ops[i][0]
+        st = max([free.get(q, 0.0)] + [end[j] + gs[3] for j in deps[i]])
+        end[i] = st + t[i]
+        free[q] = end[i] if ops[i][5] == "c" else st + 0.1
+    return max(end.values())
+
+
+def place(ops, edges, hold, keys):
+    start, busy = [0.0] * len(ops), {q: [] for q in "vstgy"}
+    for i in keys:
+        st = max([0.0] + [start[j] + x for j, x in edges[i]])
+        b, h = busy[ops[i][0]], hold[i]
+        k = len(b)
+        while k and b[k - 1][0] >= st:
+            k -= 1
+        if k and b[k - 1][1] > st:
+            st = b[k - 1][1]
+        while k < len(b) and b[k][0] < st + h - 1e-9:
+            st = b[k][1]
+            k += 1
+        b.insert(k, (st, st + h))
+        start[i] = st
+    return start
+
+
+def search(ops, deps):
+    rng = np.random.default_rng(7)
+    n, gs = len(ops), GUESS[0]
+    t = times(ops, gs)
+    hold = [t[i] if ops[i][5] == "c" else 0.1 for i in range(n)]
+    fw, prev = [], {}
+    for i in range(n):
+        e = [(j, t[j] + (0.0 if ops[i][0] == ops[j][0] == "t" else gs[3])) for j in deps[i]]
+        if ops[i][0] in "yg":
+            if ops[i][0] in prev:
+                e.append((prev[ops[i][0]], hold[prev[ops[i][0]]]))
+            prev[ops[i][0]] = i
+        fw.append(e)
+    bw = [[] for _ in range(n)]
+    for i in range(n):
+        for j, x in fw[i]:
+            bw[j].append((i, x - hold[j] + hold[i]))
+
+    def legal(key):
+        key = list(key)
+        for i in range(n):
+            key[i] = max([key[i]] + [key[j] + 1e-6 for j, _ in fw[i]])
+        return sorted(range(n), key=lambda i: (key[i], i))
+
+    def sweep(key):
+        st = place(ops, fw, hold, legal(key))
+        end = max(st[i] + t[i] for i in range(n))
+        e2 = [bw[i] + ([] if bw[i] else [(n, t[i] - hold[i])]) for i in range(n)]
+        back = place(ops + [ops[0]], e2 + [[]], hold + [0.0], [n] + legal([st[i] + hold[i] for i in range(n)])[::-1])
+        st = place(ops, fw, hold, legal([end - back[i] - hold[i] for i in range(n)]))
+        seq = legal(st)
+        return sum(span(ops, deps, seq, x) for x in GUESS), st, seq
+
+    low, best, seq = sweep([float(i) for i in range(n)])
+    for _ in range(TRIES):
+        key = list(best)
+        mid, wid, amp = rng.random() * max(best), 1.0 + 6.0 * rng.random(), 1.5 * rng.random()
+        for i in range(n):
+            if abs(best[i] - mid) < wid:
+                key[i] += float(rng.normal()) * amp
+        c, st, sq = sweep(key)
+        if c <= low:
+            low, best, seq = c, st, sq
+    ORDER["low"] = low
+    return seq
+
+
+def rank_program(g, core, T, topo):
+    rank = T.rank_of(core)
+    if rank is None:
+        return
+    n_ranks = len(T.cores)
+    if "seq" not in ORDER:
+        mid = build(T, 1, n_ranks, topo, T.cores[1])[0]
+        ORDER["seq"] = search(mid, depend(mid))
+    ops, extra = build(T, rank, n_ranks, topo, core)
+    deps = depend(ops)
+    seq = list(range(extra)) + [i + extra for i in ORDER["seq"]]
+    pos, cnt, at = {}, {}, {}
+    for k, i in enumerate(seq):
+        ch = ops[i][0] if ops[i][5] == "c" else i
+        cnt[ch] = cnt.get(ch, 0) + 1
+        pos[i], at[i] = (ch, cnt[ch]), k
+    known = {q: {} for q in "vstgy"}
+    clock, waits, marked = {}, {}, set()
+    for i in seq:
+        q = ops[i][0]
+        kn, ws = known[q], []
+        for j in sorted(deps[i], key=lambda j: -at[j]):
+            ch, p = pos[j]
+            if not (q == "t" and ch == "t") and kn.get(ch, 0) < p:
+                ws.append(j)
+                marked.add(j)
+                for c2, p2 in clock[j].items():
+                    kn[c2] = max(kn.get(c2, 0), p2)
+        waits[i] = ws
+        clock[i] = dict(kn) if ops[i][5] in ("c", "dma") else {}
+        clock[i][pos[i][0]] = pos[i][1]
+    eng = {"v": g.vector, "s": g.scalar, "t": g.tensor, "g": g, "y": g.sync}
+    count, sem, nd, sent, tail = {}, {}, 0, 0, []
+    for i in seq:
+        q, fn, _, wr, _, kind = ops[i]
+        for j in waits[i]:
+            eng[q].wait_ge(*sem[j])
+        ins = fn(g)
+        if kind == "dma":
+            sem[i] = (T.sem["dm%d" % nd], 16)
+            nd += 1
+            ins.then_inc(*sem[i])
+            if i not in marked:
+                tail.append((q, sem[i]))
+        elif kind == "c":
+            if i in marked:
+                count[q] = count.get(q, 0) + 1
+                sem[i] = (T.sem["q" + q], count[q])
+                ins.then_inc(sem[i][0], 1)
+        else:
+            sem[i] = (T.sem["ar%d" % kind[1]], NE * len(wr))
+            sent += kind[2]
+    for q, s in tail:
+        eng[q].wait_ge(*s)
+    g.wait_ge(T.sem.ls, sent)

@@ -1,42 +1,50 @@
 import numpy as np
 from concourse.bass import DstId, RemoteDMATransfer
-from concourse.mybir import AluOpType as A, AxisListType, ActivationFunctionType as F
+from concourse.mybir import AluOpType as A, ActivationFunctionType as F
 
 BIG = float(2 ** 25)
-ZN = 96
+ZN = 16
 TW = ZN + 2048
 DAYS = 3
-SEG_FIRST = [(0, 24, "S"), (24, 44, "V"), (44, 64, "V"), (64, 88, "S"), (88, 108, "V"), (108, 128, "V")]
-SEG0 = [(0, 22, "M"), (22, 48, "M"), (48, 64, "M"), (64, 88, "M"), (88, 106, "S"), (106, 128, "S")]
-SEG1 = [(0, 26, "S"), (26, 46, "V"), (46, 64, "V"), (64, 90, "S"), (90, 116, "S"), (116, 128, "V")]
-FIN = [(4, 34, "s"), (34, 64, "v"), (64, 94, "s"), (94, 124, "v")]
-TRIES = 6000
+HALF = 32767.5
+TO65536 = 1.5 * 2 ** 39
+LIFT = 811.0 * 8192
+FAR = 192
+SEG_FIRST = [(0, 44, "V"), (44, 64, "S"), (64, 114, "V"), (114, 128, "S")]
+SEG0 = [(0, 32, "M"), (32, 64, "M"), (64, 96, "X"), (96, 128, "M")]
+SEG1 = [(0, 30, "S"), (30, 64, "V"), (64, 98, "V"), (98, 128, "S")]
+SEG_LAST = SEG1
+FIN = [(4, 60, "v"), (60, 124, "s")]
+TRIES, STARTS, MOVES, SEED = 12000, 6, 10000, 2
 NE = 8
 
 SCRATCH = {}
 for dt_, bufs_ in (
         ("bfloat16", dict(E=8192, X=2048, T0=TW, T1=TW, T2=TW, D=2048, G1=2048, G2=2048, C=2048, XO=2048, XE=128, Ds=256,
-                          Cs=256, W=144, Id=128, nId=128, bF=128, b0=128, b1=128, bs=16, bd=128, neg=128, tau=136, n=128,
-                          sgn=128, nr=128, zt=128, Lc=136, cst=128)),
-        ("float32", dict(MB0=400, MB1=400, MB2=400, ZO=128, val=132, vB=128, LB=132, vr=128, df=128, d0=132, vm=128, e=128,
-                         tm=128, fp=16, own=16, m6=16, mw=16, ix=32, iq=144, iI=128, col=8, rw=64, rm=64, mk=16,
-                         mu=16, inv=16, ka=48, oz=16, oc=16, i5=16)),
-        ("int32", dict(Bt=128, vi=128, p16=128, zz=128, B=132, Bm=128, ci=128, cj=128, sm=16, sn=16, fz=16, m7=16, m8=16,
-                       m9=16, ixi=32, ik=4, i1=128, i2=128, i3=128, i4=16)),
-        ("uint16", dict(oc0=128, oc1=128, op=128, orv=128, oE=16, om=16, of=16, sP=8, sQ=8, sE=2, sZ=2, sD=16))):
+                          Cs=256, W=144, Id=128, nId=128, kId=128, hId=128, I37=128, I101=128, BO=128, bF=128, b0=128,
+                          b1=128, b2=128, bs=16, neg=64, tau=136, n=128, sgn=128, nr=128, zt=128, u=128, hi=128,
+                          cols=128, Lc=136, ka=96, m=16, mw=128, keep=128, thr=128, MB0=512, MB1=512, MB2=512)),
+        ("float32", dict(Fd=128, nFd=128, zf=136, lv=416, bb=136, rv=136, s=144, e=128, gap=16, dz=16, ZO=128, i6=128,
+                         iq=144, iI=128, col=8, rw=64, rm=64)),
+        ("int32", dict(Bt=128, B=136, Bm=128, ci=128, cj=128, sm=16, sn=16, ik=4, i1=128, i2=128, i3=128, i4=16, i5=128)),
+        ("uint16", dict(oc0=128, oc1=128, op=128, orv=128, oE=16, om=16, of=16, sP=8, sQ=8, sl=4))):
     for name_, n_ in bufs_.items():
         SCRATCH[name_] = ("sbuf", [128, n_], dt_)
-for name_ in ("pb0", "pb1", "pb2", "py0", "py1", "ps", "pv", "pw"):
+for name_ in ("pb0", "pb1", "pb2", "py0", "py1", "pv", "pz", "ps"):
     SCRATCH[name_] = ("psum", [128, 512], "float32")
-SEMAPHORES = ["qv", "qs", "qt", "qg", "ls", "ar0", "ar1", "ar2"] + ["dm%d" % i for i in range(12)]
+PIECES = dict(PA=("lv", 0), val=("lv", 128), vB=("lv", 287))
+SEMAPHORES = ["qv", "qs", "qt", "qg", "ls"] + ["ar%d" % d for d in range(DAYS)] + ["dm%d" % i for i in range(12)]
 
-GUESS = [(0.00104, 0.00162, 0.0006, 0.08, 3.0, 1.5, 0.003), (0.00088, 0.0011, 0.00045, 0.06, 2.5, 1.0, 0.0025),
-         (0.0012, 0.0021, 0.0006, 0.1, 3.5, 2.5, 0.004), (0.00104, 0.0014, 0.001, 0.08, 4.0, 1.5, 0.003)]
+GUESS = [(0.00104, 0.00134, 0.00053, 0.065, 2.4, 1.2, 0.0033, 0.035, 0.008, 0.1),
+         (0.00088, 0.0016, 0.00045, 0.06, 2.2, 2.0, 0.0028, 0.025, 0.005, 0.08),
+         (0.00104, 0.0011, 0.00062, 0.09, 2.0, 1.5, 0.003, 0.03, 0.004, 0.12),
+         (0.0012, 0.0015, 0.00062, 0.07, 2.9, 1.9, 0.0036, 0.05, 0.012, 0.06)]
 ORDER = {}
 
 
 def R(b, lo, hi, st=1):
-    return (b, lo, hi, st)
+    b, off = PIECES.get(b, (b, 0))
+    return (b, lo + off, hi + off, st)
 
 
 def build(T, rank, n_ranks, topo, core):
@@ -70,7 +78,7 @@ def build(T, rank, n_ranks, topo, core):
         ops.append([q, fn, flat(rd), flat(wr), t, kind])
 
     def vt(o, i, k, fix=0.05):
-        return (fix, n_of(i), 1) if len(i) == 2 else (fix, max(64, n_of(o) * k), 0)
+        return (fix, n_of(i), 1) if len(i) == 2 else (fix - 0.05, max(64, n_of(o) * k), 0, 1, 7)
 
     def tt(o, a, b, op):
         k = 1 if len(a) == 2 or "psum" in (SCRATCH[a[0]][0], SCRATCH[b[0]][0]) else 2
@@ -87,6 +95,7 @@ def build(T, rank, n_ranks, topo, core):
         add("v", lambda g: g.vector.tensor_copy(ap(o), ap(a)), [a], [o], vt(o, a, 1))
 
     def ms(o, c):
+        c = int(c) if SCRATCH[o[0]][2] == "int32" else float(c)
         add("v", lambda g: g.vector.memset(ap(o), c), [], [o], vt(o, o, 0.5 if two([o]) else 1))
 
     def scan(o, a, b, init, op0, op1):
@@ -94,7 +103,13 @@ def build(T, rank, n_ranks, topo, core):
             vt(o, a, 0.5 if two([o, a, b]) else 1))
 
     def act(o, a, f, **kw):
-        add("s", lambda g: g.scalar.activation(ap(o), ap(a), f, **kw), [a], [o], vt(o, a, 1, 0.065))
+        add("s", lambda g: g.scalar.activation(ap(o), ap(a), f, **kw), [a], [o], vt(o, a, 1, 0.085))
+
+    def copy(q, o, a):
+        if q == "s":
+            act(o, a, F.Copy)
+        else:
+            cp(o, a)
 
     def mms(items, start=True, stop=True):
         for k, run in enumerate(items):
@@ -102,16 +117,36 @@ def build(T, rank, n_ranks, topo, core):
                 for m, (o, l, r) in enumerate(run):
                     ins = g.tensor.matmul(ap(o), ap(l), ap(r), first and m == 0, end and m == len(run) - 1)
                 return ins
-            add("t", fn, [x for o, l, r in run for x in (l, r)], [run[0][0]],
-                (0.0, sum(max(64, n_of(r)) for o, l, r in run), 2))
+            add("t", fn, [x for o, l, r in run for x in (l, r)], [o for o, l, r in run],
+                (0.0, sum(max(64, n_of(r)) * (1 if two([r]) else 4) for o, l, r in run), 2, len(run), 8, 1, 7))
+
+    def total(o, terms, start=True, stop=True):
+        mms([[(o, l, r) for l, r in terms]], start, stop)
 
     def iota(o, pat, base, ch=0):
         kw = {} if SCRATCH[o[0]][2] == "int32" else {"allow_small_or_imprecise_dtypes": True}
-        add("g", lambda g: g.iota(ap(o), pat, base, ch, **kw), [], [o], (0.13, 2 * n_of(o), 0))
+        add("g", lambda g: g.iota(ap(o), pat, base, ch, **kw), [], [o], (0.0, 160 + 2 * n_of(o), 0))
+
+    def fill(o, c):
+        iota(o, [[0, n_of(o)]], int(c))
 
     def dma(q, o, a, rd, wr, kib):
         add(q, (lambda g: g.sync.dma_start(o, a)) if q == "y" else (lambda g: g.scalar.dma_start(o, a)), rd, wr,
-            (2.0, kib, 6), "dma")
+            (1.2, kib, 6), "dma")
+
+    def swap(buf, n, up, down, sem, first):
+        sends = ([(T.cores[rank - 1], up)] if rank > 0 else []) + ([(T.cores[rank + 1], down)] if rank < n_ranks - 1 else [])
+        sends.sort(key=lambda s: len(topo.engines(core, s[0])))
+        used, trs = [], []
+        for to, (so, do) in sends:
+            en = [x for x in topo.engines(core, to) if x not in used][:NE]
+            used += en
+            rid, pid, _ = topo.addr(to)
+            trs.append(RemoteDMATransfer(dst_ids=[DstId(rid=rid, pnc=pid)], dma_engine_mask=sum(1 << x for x in en),
+                                         remote_sem=T.sem[sem], src=T[buf][:, so:so + n], dst=T[buf][:, do:do + n]))
+        wr = ([R(buf, down[1], down[1] + n)] if rank > 0 else []) + ([R(buf, up[1], up[1] + n)] if rank < n_ranks - 1 else [])
+        add("g", lambda g: g.remote_dma_fused(trs, local_sem=T.sem.ls), [R(buf, up[0], up[0] + n), R(buf, down[0], down[0] + n)],
+            wr, (0.0, 1, 10 if first else 4), ("rem", sem, len(used)))
 
     bank = [0]
 
@@ -128,134 +163,141 @@ def build(T, rank, n_ranks, topo, core):
     def py(h):
         return R("py%d" % (h // 64), 0, 64)
 
-    P = R("col", 0, 1)
+    def px(h):
+        return R("ps" if h else "pz", 128, 192)
+
+    P, PZ, PF = R("col", 0, 1), R("col", 3, 4), R("col", 4, 5)
     Ew = R("E", 0, 8192)
-    Id, nId = L("Id"), L("nId")
-    PA, PCS, PSB = L("pv"), L("pv", 128), L("pv", 256)
+    Id, nId, kId, hId, I37, I101, Fd, nFd = (L(x) for x in ("Id", "nId", "kId", "hId", "I37", "I101", "Fd", "nFd"))
+    zw = L("zf", 8)
+    edges, twice = R("sl", 0, 1), R("sl", 2, 3)
+
+    def Z(c0, c1, st=1):
+        return R("zf", 8 + c0, 8 + c1, st)
 
     for d in range(DAYS):
         if rank == 0:
-            ms(R("MB%d" % d, 68, 136), 512.0)
+            ms(R("MB%d" % d, 128, 224), 512)
         if rank == n_ranks - 1:
-            ms(R("MB%d" % d, 0, 68), 512.0)
+            ms(R("MB%d" % d, 0, 96), -512)
     extra = len(ops)
     dma("y", T.Bt[:, :], T.boat[:, :], [], [L("Bt")], 64)
     dma("y", T.X[:, :], T.x[:, :], [], [R("X", 0, 2048)], 576)
     dma("y", T.E[:, :], T.enc[:, :], [], [Ew], 2624)
 
+    def thresholds(name, segs, less, put):
+        put(L(name), 21 - less)
+        for c0, c1, rt in segs:
+            if rt == "S":
+                put(R(name, c0, c1), 10 - less)
+        ms(R(name, 0, 128, 32), 128)
+
     iota(R("ik", 0, 1), [[0, 1]], 0, 1)
-    iota(R("i4", 0, 8), [[1, 4], [64, 2]], 0)
     iota(L("i1"), [[16, 4], [64, 32]], 0)
+    iota(R("i4", 0, 8), [[1, 4], [64, 2]], 0)
     iota(L("iI"), [[1, 128]], 0, -1)
     iota(R("iq", 0, 144), [[1, 144]], -15)
-    iota(L("i2"), [[1, 128]], 6)
-    iota(L("i3"), [[0, 4], [8192, 32]], 811)
-    iota(R("rw", 0, 8), [[-1, 2], [32, 4]], 31)
-    iota(R("rw", 8, 16), [[-1, 2], [32, 4]], 1)
+    iota(L("i2"), [[1, 128]], 0)
+    iota(L("i5"), [[0, 4], [8192, 32]], 811)
+    iota(L("cols"), [[1, 128]], 0)
+    iota(L("i6"), [[0, 8], [1, 16]], 0)
+    iota(R("rw", 0, 8), [[-31, 2], [32, 4]], 31)
+    iota(R("rw", 8, 16), [[-29, 2], [32, 4]], 30)
     iota(R("rw", 16, 32), [[1, 4], [32, 4]], 0)
-    iota(R("rw", 32, 48), [[4, 2], [0, 2], [1, 4]], 64)
+    iota(R("rw", 32, 48), [[4, 2], [0, 2], [1, 4]], 0)
     iota(R("i4", 8, 16), [[4, 8]], 0)
-    iota(R("i5", 0, 16), [[72, 2], [0, 2], [16, 4]], 0)
-    iota(R("ixi", 0, 16), [[16, 4], [4, 4]], 35)
-    iota(R("ixi", 16, 32), [[18, 2], [0, 2], [4, 4]], 0)
+    thresholds("b0", SEG0, 0, fill)
+    fill(R("ka", 0, 96), 0)
+    for d in range(DAYS):
+        k = 811 * (4 - d)
+        if d < DAYS - 1:
+            fill(R("T%d" % (d + 1), 0, ZN), 0)
+            fill(R("ka", 32 * d, 32 * d + 8), k - k % 64)
+            fill(R("ka", 32 * d + 16, 32 * d + 24), k % 64)
+        fill(R("MB%d" % d, 96, 128), 0)
+        if d == 0:
+            fill(R("bs", 0, 16), 21)
+            fill(L("zt"), 0)
+    thresholds("b2", SEG_LAST, 64, fill)
+    iota(L("i3"), [[16, 8], [0, 16]], 0)
+    thresholds("bF", SEG_FIRST, 0, ms)
+    thresholds("b1", SEG1, 64, ms)
+    for r, c in ((R("T0", 0, ZN), 0), (R("B", 0, 1), 0), (R("neg", 0, 64), -1), (R("val", 128, 129), 0), (R("bb", 128, 129), 0),
+                 (R("rv", 0, 1), -65536), (R("tau", 128, 129), BIG), (R("Lc", 0, 1), 0), (R("pv", 0, 1), 0),
+                 (R("s", 64, 137, 72), 0), (R("m", 0, 16), 0)):
+        ms(r, c)
     ts(R("ik", 1, 2), R("ik", 0, 1), 15, None, A.bitwise_and)
     ts(R("ik", 2, 3), R("ik", 0, 1), 112, None, A.bitwise_and)
     cp(R("col", 0, 2), R("ik", 1, 3))
     ts(R("col", 2, 3), P, 4.0, None, A.mult)
+    ts(PZ, P, float(ZN), None, A.add)
+    ts(PF, P, float(FAR), None, A.add)
     ts(R("sP", 0, 8), R("i4", 0, 8), R("col", 2, 3), None, A.add)
     ts(L("op"), L("i1"), P, None, A.add)
-    ts(Id, L("iI"), 0.0, None, A.is_equal)
-    ts(nId, L("iI"), 0.0, -1.0, A.is_equal, A.mult)
+    for mat, w in ((Id, 1.0), (nId, -1.0), (hId, BIG / 2), (kId, -32 * BIG), (I37, 37.0), (I101, 101.0), (Fd, 1.0), (nFd, -1.0)):
+        ts(mat, L("iI"), 0.0, w, A.is_equal, A.mult)
     ts(R("W", 0, 144), R("iq", 0, 144), R("col", 1, 2), -BIG, A.is_equal, A.mult)
-    ts(R("i2", 0, 128, 32), R("i2", 0, 128, 32), 26.0, 1.0 / 32, A.add, A.mult)
-    ts(PCS, L("i2"), 65536.0, None, A.mult)
-    cp(L("cst"), L("i2"))
-    ms(R("cst", 31, 128, 32), 0.0)
-    cp(PSB, L("i3"))
-    ts(R("mk", 0, 16), R("iq", 15, 31), P, None, A.is_equal)
-    for k in range(3):
-        tt(R("rm", 16 * k, 16 * k + 16), R("rw", 16 * k, 16 * k + 16), R("mk", 0, 16), A.mult)
-        add("v", lambda g, k=k: g.vector.tensor_reduce(T.col[:, 3 + k:4 + k], T.rm[:, 16 * k:16 * k + 16], AxisListType.X, A.add),
-            [R("rm", 16 * k, 16 * k + 16)], [R("col", 3 + k, 4 + k)], (0.05, 64, 0))
-    cp(R("sE", 0, 1), R("col", 3, 4))
-    ts(R("sQ", 0, 8), R("i4", 8, 16), R("col", 4, 5), None, A.add)
-    cp(R("sZ", 0, 1), R("col", 5, 6))
-    ts(R("sD", 0, 16), R("i5", 0, 16), P, None, A.add)
-    ts(R("ix", 0, 32), R("ixi", 0, 32), 65536.0, None, A.mult)
-    for name, segs, heads in (("bF", SEG_FIRST, True), ("b0", SEG0, True), ("b1", SEG1, False)):
-        ms(L(name), 10.5 * BIG)
-        runs = []
-        for c0, c1, rt in segs:
-            if rt == "S":
-                if runs and runs[-1][1] == c0:
-                    runs[-1][1] = c1
-                else:
-                    runs.append([c0, c1])
-        for c0, c1 in runs:
-            ms(R(name, c0, c1), 5.0 * BIG)
-        if heads:
-            ms(R(name, 0, 128, 32), 64.0 * BIG)
-    ms(R("bs", 0, 16), 10.5 * BIG)
-    ms(L("neg"), -1.0)
-    ms(L("zt"), 0.0)
-    ms(R("tau", 128, 136), BIG)
-    ms(R("Lc", 0, 1), 0.0)
-    ms(R("val", 0, 132, 129), 0.0)
-    ms(R("LB", 0, 1), 0.0)
-    ms(R("d0", 128, 129), 0.0)
-    ms(R("B", 0, 1), 0)
-    ms(R("pw", 0, 1), 0.0)
-    ms(R("pw", 336, 409, 72), 0.0)
-    for d in range(DAYS):
-        ms(R("T%d" % d, 0, ZN), 512.0)
-        if d < DAYS - 1:
-            ms(R("ka", 16 * d, 16 * d + 16), float(811 * (2 * DAYS + d)))
-            ms(R("ka", 16 * d + 4, 16 * d + 12), float(811 * (2 * d + 2)))
-    ms(R("mu", 0, 8), 101.0)
-    ms(R("mu", 8, 16), 37.0)
-    ms(R("inv", 0, 8), 1.0 / 37)
-    ms(R("inv", 8, 16), 1.0 / 101)
+    ts(L("BO"), L("i3"), R("col", 1, 2), None, A.is_equal)
+    ts(L("pv", 128), L("i2"), 65536.0, None, A.mult)
+    cp(L("pv", 256), L("i5"))
+    ts(L("keep"), L("i6"), P, None, A.is_equal)
+    tt(R("rm", 0, 48), R("rw", 0, 48), R("keep", 0, 48), A.mult)
+    ts(L("thr"), L("keep"), -64.0, 74.5, A.mult, A.add)
+    ts(L("keep"), L("i6"), 0.0, None, A.not_equal)
+    scan(R("rw", 0, 48), R("keep", 0, 48), R("rm", 0, 48), 0.0, A.mult, A.add)
+    cp(R("sl", 0, 3), R("rw", 15, 48, 16))
+    ts(R("sQ", 0, 8), R("i4", 8, 16), R("rw", 31, 32), None, A.add)
 
-    def reduce(y, bias, cb, c0, c1, dyn=None, stop=True):
-        mms([[(y, Id, bias)] + ([(y, nId, dyn)] if dyn else [])
-             + [(y, R("W", 15 - p, 143 - p), R(cb, 16 * c0 + p, 16 * c1, 16)) for p in range(16)]], True, stop)
+    def opening(h, name, left=None):
+        total(py(h), [(hId, R(name, h, h + 64))] + ([(kId, R(left, h, h + 64))] if left else []), True, False)
 
-    def numbers(t, h, w):
-        ts(R("pv", h, h + w), R("zz", h, h + w), 37.0, float(811 * t), A.mult, A.add)
-        ts(R("B", h + 1, h + w + 1), R("zz", h, h + w), 101.0, None, A.mult)
-        tt(R("ci", h, h + w), R("pv", h, h + w), R("B", h, h + w), A.add)
-        ts(R("cj", h, h + w), R("ci", h, h + w), 8191, None, A.bitwise_and)
-        cp(R("oc0", h, h + w), R("cj", h, h + w))
+    def reduce(y, cb, c0, c1, stop=True):
+        total(y, [(R("W", 15 - p, 143 - p), R(cb, 16 * c0 + p, 16 * c1, 16)) for p in range(16)], False, stop)
 
-    def values():
-        tt(L("val", 1), L("zz"), PCS, A.add)
+    def columns(o, mine, rival, a, b, c0, c1):
+        if isinstance(rival, tuple):
+            tt(R(a, c0, c1), mine, rival, A.add)
+        else:
+            ts(R(a, c0, c1), mine, rival, None, A.add)
+        ts(R(b, c0, c1), R(a, c0, c1), 8191, None, A.bitwise_and)
+        cp(R(o, c0, c1), R(b, c0, c1))
+
+    def morning(t, c0, c1):
+        ts(R("PA", c0, c1), Z(c0, c1), 37.0, 37 * HALF + 811 * t + LIFT, A.mult, A.add)
+        ts(R("B", c0 + 1, c1 + 1), Z(c0, c1), 101.0, 101 * HALF, A.mult, A.add)
+        columns("oc0", R("PA", c0, c1), R("B", c0, c1), "ci", "cj", c0, c1)
+
+    def values(patched):
         ts(L("Bm"), L("B", 1), 8191, None, A.bitwise_and)
-        tt(L("vB"), L("Bm"), PSB, A.add)
+        tt(L("vB"), L("Bm"), L("pv", 256), A.add)
+        tt(L("val"), Z(0, 128), L("pv", 128), A.add)
+        if patched:
+            act(R("vB", 0, 128, 32), Z(0, 128, 32), F.Identity, scale=101.0, bias=101 * HALF + 811.0 - LIFT)
 
-    def halves(done, bias, dyn=None, stop=True):
+    def halves(done, stop=True):
         if done in (64, 128):
-            h = done - 64
-            reduce(py(h), R(bias, h, done), "C", h, done, dyn and R(dyn, h, done), stop)
+            reduce(py(done - 64), "C", done - 64, done, stop)
 
     def race(rt, c0, c1, eg, xs, xq):
         q = pb(16 * (c1 - c0))
-        if rt == "M":
-            mms([[(q, Id, xq), (q, nId, xs)]])
-            act(wide("D", c0, c1), q, F.Copy)
-            tt(wide("C", c0, c1), eg, wide("D", c0, c1), A.is_gt)
-        else:
+        if rt == "S":
             act(wide("G1", c0, c1), eg, F.Copy)
             mms([[(q, nId, xq), (q, Id, xs)], [(q, Id, wide("G1", c0, c1))]])
             act(wide("C", c0, c1), q, F.Sign, bias=-0.5)
+        else:
+            total(q, [(Id, xq), (nId, xs)])
+            act(wide("D", c0, c1), q, F.Copy)
+            tt(wide("C", c0, c1), eg, wide("D", c0, c1), A.is_gt)
 
-    cp(L("zz"), (L("Bt"), R("sP", 0, 8)))
-    numbers(0, 0, 128)
-    values()
-    act(R("T0", 16, 80), R("X", 0, 64), F.Copy)
+    ts(zw, (L("Bt"), R("sP", 0, 8)), -HALF, None, A.add)
+    morning(0, 0, 128)
+    values(False)
+    for h in (0, 64):
+        opening(h, "bF")
     for c0 in range(0, 128, 32):
         act(wide("T0", c0, c0 + 32, ZN), (R("X", 0, 2048), R("op", c0, c0 + 32)), F.Copy)
         q = pb(512)
-        mms([[(q, Id, wide("T0", c0 - 1, c0 + 31, ZN)), (q, nId, wide("T0", c0, c0 + 32, ZN))]])
+        total(q, [(Id, wide("T0", c0 - 1, c0 + 31, ZN)), (nId, wide("T0", c0, c0 + 32, ZN))])
         act(wide("D", c0, c0 + 32), q, F.Copy)
     for c0, c1, rt in SEG_FIRST:
         eg = (Ew, R("oc0", c0, c1))
@@ -266,7 +308,7 @@ def build(T, rank, n_ranks, topo, core):
             q = pb(16 * (c1 - c0))
             mms([[(q, nId, wide("D", c0, c1))], [(q, Id, wide("G1", c0, c1))]])
             act(wide("C", c0, c1), q, F.Sign, bias=-0.5)
-        halves(c1, "bF")
+        halves(c1)
 
     for d in range(DAYS):
         Tn, Tx, MB, last = "T%d" % d, "T%d" % (d + 1), "MB%d" % d, d == DAYS - 1
@@ -274,16 +316,20 @@ def build(T, rank, n_ranks, topo, core):
         for h in (0, 64):
             scan(R("tau", h, h + 64), R("neg", 0, 64), py(h), 1.0, A.mult, A.max)
         tt(L("n"), L("tau"), L("tau", 1), A.min)
-        scan(L("Lc", 1), L("n"), L("cst"), 0.0, A.max, A.min)
-        ts(L("orv"), L("Lc"), 16.0, P, A.mult, A.add)
-        scan(L("LB", 1), L("n"), L("vB"), 0.0, A.max, A.min)
-        tt(L("ci"), PA, L("LB"), A.add)
-        ts(L("cj"), L("ci"), 8191, None, A.bitwise_and)
-        cp(L("oc1"), L("cj"))
+        scan(L("Lc", 1), L("n"), L("cols"), 0.0, A.max, A.min)
+        ts(L("orv"), L("Lc"), 16.0, PZ, A.mult, A.add)
+        scan(R("pv", 1, 128), R("n", 0, 127), R("vB", 0, 127), 0.0, A.max, A.min)
+        columns("oc1", L("PA"), L("pv"), "ci", "cj", 0, 128)
         act(L("sgn"), L("n"), F.Sign, scale=-1.0)
-        act(L("bd"), L("n"), F.Relu, scale=-128.0)
         act(L("nr"), L("sgn"), F.Relu)
-        for c0, c1, rt in SEG1:
+        for h in (0, 64):
+            opening(h, "b2" if last else "b1", "sgn")
+        scan(L("rv", 1), L("n"), L("val"), -65536.0, A.max, A.min)
+        tt(L("pv", 384), L("rv", 1), L("rv"), A.subtract)
+        scan(L("bb"), L("tau"), L("val"), 0.0, A.max, A.min)
+        for h in (0, 64):
+            total(px(h), [(Fd, R("bb", h, h + 64)), (nFd, R("bb", h + 1, h + 65)), (Fd, R("val", h + 1, h + 65))], True, False)
+        for c0, c1, rt in SEG_LAST if last else SEG1:
             eg, xr, xs = (Ew, R("oc1", c0, c1)), (Tw, R("orv", c0, c1)), wide(Tn, c0, c1, ZN)
             if rt == "V":
                 tt(wide("D", c0, c1), eg, xs, A.add)
@@ -291,115 +337,94 @@ def build(T, rank, n_ranks, topo, core):
             else:
                 act(wide("G2", c0, c1), xr, F.Copy)
                 race(rt, c0, c1, eg, xs, wide("G2", c0, c1))
-            halves(c1, "b1", "bd")
-        scan(L("pw", 1), L("n"), L("val", 1), 0.0, A.max, A.min)
-        tt(L("vr"), L("val", 1), L("n"), A.min)
-        tt(L("df"), L("pw"), L("vr"), A.subtract)
-        tt(L("pw", 136), L("val"), L("tau"), A.max)
-        tt(L("pv", 384), L("pw", 136), L("val", 1), A.min)
-        tt(L("d0"), L("pv", 384), L("val", 1), A.subtract)
-        tt(L("vm"), L("pv", 384), L("d0", 1), A.subtract)
+            halves(c1)
         for h in (0, 64):
-            def H(b, lo=0, st=1):
-                return R(b, lo + h, lo + h + 64, st)
-            s0 = 272 + h // 8
-            scan(H("pw", 136), H("sgn"), py(h), BIG, A.mult, A.max)
-            tt(H("e"), H("pw", 136), H("df"), A.max)
-            scan(H("pw", s0, -1), H("nr", 0, -1), H("e", 0, -1), 0.0, A.mult, A.min)
-            tt(H("tm"), H("pw", s0), H("vm"), A.add)
-            tt(H("vi"), H("tm"), H("pw", s0 + 1), A.subtract)
-            ts(H("p16"), H("vi"), 12, 0xFF0, A.arith_shift_right, A.bitwise_and)
-            ts(H("zz"), H("vi"), 65535, None, A.bitwise_and)
+            def H(b, sh=0, st=1):
+                return R(b, h + sh, h + 64 + sh, st)
+            pad = h // 8
+            scan(H("u"), py(h), H("sgn"), 0.0, A.max, A.mult)
+            tt(H("e"), H("u"), H("pv", 384), A.min)
+            scan(H("s", pad, -1), H("nr", 0, -1), H("e", 0, -1), 0.0, A.mult, A.max)
+            total(px(h), [(nFd, H("s", pad)), (Fd, H("s", pad + 1))], False, True)
+            ts(H("hi"), px(h), TO65536, TO65536, A.add, A.subtract)
             if not last:
-                ts(H("op"), H("p16"), P, None, A.add)
-                numbers(2 * d + 2, h, 64)
-        ts(R("oE", 0, 16), (L("p16"), R("sE", 0, 1)), P, None, A.add)
-        ts(R(MB, 136, 140), R("zz", 31, 128, 32), 101.0, None, A.mult)
-        oh = 204 if last else 332
-        ts(R(MB, oh + 64, oh + 68), R("zz", 0, 128, 32), 37.0, None, A.mult)
-        act(R(MB, 140, 204), (Tw, R("oE", 0, 4)), F.Copy)
-        act(R(MB, oh, oh + 64), (Tw, R("oE", 12, 16)), F.Copy, scale=-1.0)
-        sends = []
-        if rank > 0:
-            sends.append((T.cores[rank - 1], oh, 0))
-        if rank < n_ranks - 1:
-            sends.append((T.cores[rank + 1], 136, 68))
-        sends.sort(key=lambda s: len(topo.engines(core, s[0])))
-        used, trs = [], []
-        for dst, so, do in sends:
-            en = [x for x in topo.engines(core, dst) if x not in used][:NE]
-            used += en
-            rid, pid, _ = topo.addr(dst)
-            trs.append(RemoteDMATransfer(dst_ids=[DstId(rid=rid, pnc=pid)], dma_engine_mask=sum(1 << x for x in en),
-                                         remote_sem=T.sem["ar%d" % d], src=T[MB][:, so:so + 68], dst=T[MB][:, do:do + 68]))
-        wr = ([R(MB, 68, 136)] if rank > 0 else []) + ([R(MB, 0, 68)] if rank < n_ranks - 1 else [])
-        add("g", lambda g, trs=trs: g.remote_dma_fused(trs, local_sem=T.sem.ls), [R(MB, 136, 204), R(MB, oh, oh + 68)], wr,
-            (0.0, 1, 4 if d else 7), ("rem", d, len(used)))
-        if not last:
-            act(R(MB, 204, 268), (Tw, R("oE", 4, 8)), F.Copy)
-            act(R(MB, 268, 332), (Tw, R("oE", 8, 12)), F.Copy, scale=-1.0)
-            tt(R("own", 0, 16), (L("zz"), R("sE", 0, 1)), R("ix", 0, 16), A.add)
-            tt(R("oz", 0, 16), (L("zz"), R("sE", 0, 1)), R("mu", 0, 16), A.mult)
-            tt(R("oc", 0, 16), R("oz", 0, 16), R("ka", 16 * d, 16 * d + 16), A.add)
+                ts(H("op"), H("hi"), 2.0 ** -12, PZ, A.mult, A.add)
+            tt(Z(h, h + 64), px(h), H("hi"), A.subtract)
+            if not last:
+                opening(h, "b0")
+                morning(2 * d + 2, h, h + 64)
+        nb = 8 if last else 16
+
+        def M(lo, n=4):
+            return R(MB, lo, lo + n)
+
+        def S(lo, n=4):
+            return R("ps", lo, lo + n)
+        ts(R("oE", 0, 16), (L("hi"), edges), 2.0 ** -12, PZ, A.mult, A.add)
+        cp(M(288, 16), (zw, edges))
+        tt(M(304, 16), (zw, edges), M(288, 16), A.subtract)
+        act(M(224, 64), (Tw, R("oE", 0, 4)), F.Copy)
+        act(M(320, 64), (Tw, R("oE", 4, 8)), F.Copy)
+        swap(MB, 96, (288, 0), (224, 128), "ar%d" % d, d == 0)
+        own = [(S(4 * k), (I101, I37)[k % 2], M(288 + 16 * j + 4 * k)) for k in range(nb // 4) for j in range(2)]
+        far = [(S(4 * k), (I37, I101)[k % 2], M((4, 192)[k % 2] + 16 * j)) for k in range(nb // 4) for j in range(2)]
+        mms([[(S(0, nb), Id, R("ka", 32 * d, 32 * d + nb))] + own], True, False)
+        if last:
+            ts(L("op"), (L("hi"), R("sQ", 0, 8)), 2.0 ** -12, PZ, A.mult, A.add)
+            for c0, c1, q in FIN:
+                copy(q, wide("XO", c0, c1), (Tw, R("op", c0, c1)))
+                dma("y", T.yx[:, 16 * c0:16 * c1], T.XO[:, 16 * c0:16 * c1], [wide("XO", c0, c1)], [], 256)
+            ts(L("ZO"), (zw, R("sQ", 0, 8)), HALF, None, A.add)
+        else:
+            act(M(384, 128), (Tw, R("oE", 8, 16)), F.Copy)
+            values(True)
             for c0, c1, rt in SEG0:
                 xs = wide(Tx, c0, c1, ZN)
-                act(xs, (Tw, R("op", c0, c1)), F.Copy)
+                copy("v" if rt == "X" else "s", xs, (Tw, R("op", c0, c1)))
                 race(rt, c0, c1, (Ew, R("oc0", c0, c1)), xs, wide(Tx, c0 - 1, c1 - 1, ZN))
-                halves(c1, "b0", None, False)
-        else:
-            k = float(811 * (2 * DAYS + d))
-            ts(R("oc", 4, 8), R(MB, 136, 140), k, None, A.add)
-            ts(R("oc", 8, 12), R(MB, 268, 272), k, None, A.add)
-            tt(R("own", 4, 8), R("zz", 31, 128, 32), R("ix", 0, 4), A.add)
-            tt(R("own", 8, 12), R("zz", 0, 128, 32), R("ix", 4, 8), A.add)
-            ts(L("op"), (L("p16"), R("sQ", 0, 8)), P, None, A.add)
-            for c0, c1, q in FIN:
-                src = (Tw, R("op", c0, c1))
-                if q == "s":
-                    act(wide("XO", c0, c1), src, F.Copy)
-                else:
-                    cp(wide("XO", c0, c1), src)
-            dma("y", T.yx[:, 64:1024], T.XO[:, 64:1024], [R("XO", 64, 1024)], [], 256)
-            dma("y", T.yx[:, 1024:1984], T.XO[:, 1024:1984], [R("XO", 1024, 1984)], [], 256)
-            cp(L("ZO"), (L("zz"), R("sQ", 0, 8)))
-        fz = (R(MB, 0, 136), R("sZ", 0, 1))
-        tt(R("sm", 0, 16), fz, R("oc", 0, 16), A.add)
-        a, b = (4, 12) if last else (0, 16)
-        ts(R("sn", a, b), R("sm", a, b), 8191, None, A.bitwise_and)
-        cp(R("om", a, b), R("sn", a, b))
-        tt(wide("Ds", a, b), (R(MB, 0, 136), R("sD", a, b)), R(MB, 140, 140 + 16 * (b - a)), A.add)
-        tt(wide("Cs", a, b), (Ew, R("om", a, b)), wide("Ds", a, b), A.is_gt)
-        reduce(R("ps", a, b), R("bs", a, b), "Cs", a, b)
-        tt(R("fz", 0, 16), fz, R("inv", 0, 16), A.mult)
-        tt(R("fp", 0, 16), R("fz", 0, 16), R("ix", 16, 32), A.add)
-        tt(R("m6", a, b), R("ps", a, b), R("fp", a, b), A.max)
-        tt(R("m7", a, b), R("m6", a, b), R("own", a, b), A.min)
-        ts(R("m8", a, b), R("m7", a, b), 14, 0x1FC, A.arith_shift_right, A.bitwise_and)
-        if not last:
-            ts(R("mw", 0, 16), R("ps", 0, 16), 0.0, 128.0, A.is_lt, A.mult)
-            tt(R("zt", 31, 128, 32), R("ps", 4, 8), R("mw", 0, 4), A.mult)
-            tt(R("zt", 1, 128, 32), R("ps", 8, 12), R("mw", 12, 16), A.mult)
-            for h in (0, 64):
-                mms([[(py(h), Id, R("zt", h, h + 64))]], False, True)
-            ts(R("of", 0, 8, 2), R("m8", 0, 4), P, None, A.add)
-            ts(R("of", 12, 16), R("m8", 12, 16), P, None, A.add)
-            act(R(Tx, 16, 80), (R(MB, 0, 400), R("of", 12, 16)), F.Abs)
-            for lq in range(4):
-                act(wide(Tx, 32 * lq + 31, 32 * lq + 32, ZN), (R(MB, 0, 400), R("of", 2 * lq, 2 * lq + 1)), F.Abs)
-            ts(R("zz", 31, 128, 32), R("m7", 0, 4), 65535, None, A.bitwise_and)
-            ts(R("zz", 0, 128, 32), R("m7", 12, 16), 65535, None, A.bitwise_and)
-            ts(R("B", 1, 129, 32), R("zz", 0, 128, 32), 101.0, None, A.mult)
-            ts(R("pv", 31, 128, 32), R("zz", 31, 128, 32), 37.0, float(811 * (2 * d + 2)), A.mult, A.add)
-            values()
-        else:
-            ts(R("of", 4, 12), R("m8", 4, 12), P, None, A.add)
-            act(L("XE"), (R(MB, 0, 272), R("of", 4, 12)), F.Abs)
+                halves(c1, False)
+        mms([far + [(S(0, nb), Id, R("ka", 32 * d + 16, 32 * d + 16 + nb))]], False, True)
+        columns("om", S(0, nb), 138 * HALF + 811 * (2 * DAYS + d if last else 2 * d + 2), "sm", "sn", 0, nb)
+        q = pb(16 * nb)
+        for k, (ahead, behind) in enumerate(((224, 32), (128, 320), (384, 32), (128, 448))[:nb // 4]):
+            total(R(q[0], 64 * k, 64 * k + 64), [(Id, M(ahead, 64)), (nId, M(behind, 64))])
+        act(wide("Ds", 0, nb), q, F.Copy)
+        tt(wide("Cs", 0, nb), (Ew, R("om", 0, nb)), wide("Ds", 0, nb), A.is_gt)
+        gap = R(q[0], 256, 264)
+        mms([[(gap, Id, M(288, 8))] + [(R(q[0], 256 + 4 * k, 260 + 4 * k), nId, M((4, 192)[k] + 16 * j))
+                                       for k in range(2) for j in range(2)] + [(gap, Id, M(304, 8))]])
+        if last:
+            cnt = pb(128)
+            total(cnt, [(L("BO"), wide("Cs", 0, 8))])
+            ts(L("mw"), cnt, 10.5, None, A.is_gt)
+            tt(L("u"), cnt, L("thr"), A.is_gt)
+            tt(L("pv"), L("mw"), q, A.mult)
+            tt(R("XE", 0, 64), M(224, 64), R("pv", 0, 64), A.subtract)
+            tt(R("XE", 64, 128), M(320, 64), R("pv", 64, 128), A.add)
             dma("s", T.yx[:, 0:64], T.XE[:, 64:128], [R("XE", 64, 128)], [], 16)
             dma("y", T.yx[:, 1984:2048], T.XE[:, 0:64], [R("XE", 0, 64)], [], 16)
-            ts(R("m9", 4, 12), R("m7", 4, 12), 65535, None, A.bitwise_and)
-            cp(R("ZO", 124, 128), R("m9", 4, 8))
-            cp(R("ZO", 0, 4), R("m9", 8, 12))
+            scan(L("n"), L("keep"), L("u"), 0.0, A.mult, A.add)
+            tt(R("dz", 0, 8), gap, R("n", 15, 128, 16), A.mult)
+            tt(R("ZO", 124, 128), R("ZO", 124, 128), R("dz", 0, 4), A.subtract)
+            tt(R("ZO", 0, 4), R("ZO", 0, 4), R("dz", 4, 8), A.subtract)
             dma("y", T.yb[:, :], T.ZO[:, :], [L("ZO")], [], 64)
+            break
+        for k, w in enumerate((37.0, 1.0, 101.0, 1.0)):
+            act(R("gap", 4 * k, 4 * k + 4), R(q[0], 256 + 4 * (k // 2), 260 + 4 * (k // 2)), F.Copy, scale=w)
+        total(S(16, 16), [(hId, R("bs", 0, 16))], True, False)
+        reduce(S(16, 16), "Cs", 0, 16)
+        ts(R("m", 0, 8), S(16, 8), 0.0, -1.0, A.is_lt, A.mult)
+        tt(R("zt", 31, 128, 32), S(24), R("m", 0, 4), A.mult)
+        tt(R("zt", 1, 128, 32), S(28), R("m", 4, 8), A.mult)
+        for h in (0, 64):
+            total(py(h), [(kId, R("zt", h, h + 64))], False, True)
+        tt(R("dz", 0, 16), (R("m", 0, 16), twice), R("gap", 0, 16), A.mult)
+        tt(R("lv", 31, 415, 32), R("lv", 31, 415, 32), R("dz", 0, 12), A.add)
+        tt(R("val", 0, 128, 32), R("val", 0, 128, 32), R("dz", 12, 16), A.add)
+        ts(R("of", 0, 16, 2), R("m", 0, 8), float(FAR), PF, A.mult, A.add)
+        for k in range(8):
+            lo, c = (32, 128)[k // 4] + 16 * (k % 4), 32 * (k % 4) + (31, 0)[k // 4]
+            act(wide(Tx, c, c + 1, ZN), (M(lo, FAR + 16), R("of", 2 * k, 2 * k + 1)), F.Copy)
     return ops, extra
 
 
@@ -437,14 +462,18 @@ def depend(ops):
 
 def times(ops, gs):
     gs = list(gs) + [gs[4] + gs[5]]
-    return [o[4][0] + o[4][1] * gs[o[4][2]] for o in ops]
+    return [o[4][0] + sum(n * gs[k] for n, k in zip(o[4][1::2], o[4][2::2])) for o in ops]
+
+
+def lag(ops, i, j, gs):
+    return gs[3] if ops[j][0] != "t" else 0.0 if ops[i][0] == "t" else gs[3] + gs[9]
 
 
 def span(ops, deps, seq, gs):
     t, free, end = times(ops, gs), {}, {}
     for i in seq:
         q = ops[i][0]
-        st = max([free.get(q, 0.0)] + [end[j] + gs[3] for j in deps[i]])
+        st = max([free.get(q, 0.0)] + [end[j] + lag(ops, i, j, gs) for j in deps[i]])
         end[i] = st + t[i]
         free[q] = end[i] if ops[i][5] == "c" else st + 0.1
     return max(end.values())
@@ -469,13 +498,13 @@ def place(ops, edges, hold, keys):
 
 
 def search(ops, deps):
-    rng = np.random.default_rng(7)
+    rng = np.random.default_rng(SEED)
     n, gs = len(ops), GUESS[0]
     t = times(ops, gs)
     hold = [t[i] if ops[i][5] == "c" else 0.1 for i in range(n)]
     fw, prev = [], {}
     for i in range(n):
-        e = [(j, t[j] + (0.0 if ops[i][0] == ops[j][0] == "t" else gs[3])) for j in deps[i]]
+        e = [(j, t[j] + lag(ops, i, j, gs)) for j in deps[i]]
         if ops[i][0] in "yg":
             if ops[i][0] in prev:
                 e.append((prev[ops[i][0]], hold[prev[ops[i][0]]]))
@@ -485,6 +514,19 @@ def search(ops, deps):
     for i in range(n):
         for j, x in fw[i]:
             bw[j].append((i, x - hold[j] + hold[i]))
+    known = [(times(ops, x), [[(j, lag(ops, i, j, x)) for j in deps[i]] for i in range(n)]) for x in GUESS]
+
+    def spans(seq):
+        out = 0.0
+        for tx, ex in known:
+            free, end = {}, [0.0] * n
+            for i in seq:
+                q = ops[i][0]
+                st = max([free.get(q, 0.0)] + [end[j] + x for j, x in ex[i]])
+                end[i] = st + tx[i]
+                free[q] = end[i] if ops[i][5] == "c" else st + 0.1
+            out += max(end)
+        return out
 
     def legal(key):
         key = list(key)
@@ -499,18 +541,32 @@ def search(ops, deps):
         back = place(ops + [ops[0]], e2 + [[]], hold + [0.0], [n] + legal([st[i] + hold[i] for i in range(n)])[::-1])
         st = place(ops, fw, hold, legal([end - back[i] - hold[i] for i in range(n)]))
         seq = legal(st)
-        return sum(span(ops, deps, seq, x) for x in GUESS), st, seq
+        return spans(seq), st, seq
 
-    low, best, seq = sweep([float(i) for i in range(n)])
-    for _ in range(TRIES):
-        key = list(best)
-        mid, wid, amp = rng.random() * max(best), 1.0 + 6.0 * rng.random(), 1.5 * rng.random()
-        for i in range(n):
-            if abs(best[i] - mid) < wid:
-                key[i] += float(rng.normal()) * amp
-        c, st, sq = sweep(key)
-        if c <= low:
-            low, best, seq = c, st, sq
+    def shake(state, tries):
+        for _ in range(tries):
+            key = list(state[1])
+            mid, wid, amp = rng.random() * max(key), 1.0 + 6.0 * rng.random(), 1.5 * rng.random()
+            new = sweep([x + float(rng.normal()) * amp if abs(x - mid) < wid else x for x in key])
+            if new[0] <= state[0]:
+                state = new
+        return state
+
+    first = sweep([float(i) for i in range(n)])
+    low, _, seq = shake(min(shake(first, TRIES // (2 * STARTS)) for _ in range(STARTS)), TRIES // 2)
+    for _ in range(MOVES):
+        at = {x: k for k, x in enumerate(seq)}
+        k = int(rng.integers(n))
+        i = seq[k]
+        lo = max([k - 12, 0] + [at[j] + 1 for j, _ in fw[i]])
+        hi = min([k + 12, n - 1] + [at[j] - 1 for j, _ in bw[i]])
+        to = int(rng.integers(lo, hi + 1))
+        if any(ops[x][0] == ops[i][0] for x in seq[min(k, to):max(k, to) + 1] if x != i):
+            new = seq[:k] + seq[k + 1:]
+            new.insert(to, i)
+            c = spans(new)
+            if c <= low:
+                low, seq = c, new
     ORDER["low"] = low
     return seq
 
@@ -565,7 +621,7 @@ def rank_program(g, core, T, topo):
                 sem[i] = (T.sem["q" + q], count[q])
                 ins.then_inc(sem[i][0], 1)
         else:
-            sem[i] = (T.sem["ar%d" % kind[1]], NE * len(wr))
+            sem[i] = (T.sem[kind[1]], NE * len(wr))
             sent += kind[2]
     for q, s in tail:
         eng[q].wait_ge(*s)

import numpy as np
from concourse.bass import DstId, RemoteDMATransfer
from concourse.mybir import AluOpType as A, ActivationFunctionType as F

BIG = float(2 ** 25)
ZN = 16
TW = ZN + 2048
DAYS = 3
HALF = 32767.5
TO65536 = 1.5 * 2 ** 39
LIFT = 811.0 * 8192
FAR = 192
SEG_FIRST = [(0, 44, "V"), (44, 64, "S"), (64, 114, "V"), (114, 128, "S")]
SEG0 = [(0, 32, "M"), (32, 64, "M"), (64, 96, "X"), (96, 128, "M")]
SEG1 = [(0, 30, "S"), (30, 64, "V"), (64, 98, "V"), (98, 128, "S")]
SEG_LAST = SEG1
FIN = [(4, 60, "v"), (60, 124, "s")]
TRIES, STARTS, MOVES, SEED = 12000, 6, 10000, 2
NE = 8

SCRATCH = {}
for dt_, bufs_ in (
        ("bfloat16", dict(E=8192, X=2048, T0=TW, T1=TW, T2=TW, D=2048, G1=2048, G2=2048, C=2048, XO=2048, XE=128, Ds=256,
                          Cs=256, W=144, Id=128, nId=128, kId=128, hId=128, I37=128, I101=128, BO=128, bF=128, b0=128,
                          b1=128, b2=128, bs=16, neg=64, tau=136, n=128, sgn=128, nr=128, zt=128, u=128, hi=128,
                          cols=128, Lc=136, ka=96, m=16, mw=128, keep=128, thr=128, MB0=512, MB1=512, MB2=512)),
        ("float32", dict(Fd=128, nFd=128, zf=136, lv=416, bb=136, rv=136, s=144, e=128, gap=16, dz=16, ZO=128, i6=128,
                         iq=144, iI=128, col=8, rw=64, rm=64)),
        ("int32", dict(Bt=128, B=136, Bm=128, ci=128, cj=128, sm=16, sn=16, ik=4, i1=128, i2=128, i3=128, i4=16, i5=128)),
        ("uint16", dict(oc0=128, oc1=128, op=128, orv=128, oE=16, om=16, of=16, sP=8, sQ=8, sl=4))):
    for name_, n_ in bufs_.items():
        SCRATCH[name_] = ("sbuf", [128, n_], dt_)
for name_ in ("pb0", "pb1", "pb2", "py0", "py1", "pv", "pz", "ps"):
    SCRATCH[name_] = ("psum", [128, 512], "float32")
PIECES = dict(PA=("lv", 0), val=("lv", 128), vB=("lv", 287))
SEMAPHORES = ["qv", "qs", "qt", "qg", "ls"] + ["ar%d" % d for d in range(DAYS)] + ["dm%d" % i for i in range(12)]

GUESS = [(0.00104, 0.00134, 0.00053, 0.065, 2.4, 1.2, 0.0033, 0.035, 0.008, 0.1),
         (0.00088, 0.0016, 0.00045, 0.06, 2.2, 2.0, 0.0028, 0.025, 0.005, 0.08),
         (0.00104, 0.0011, 0.00062, 0.09, 2.0, 1.5, 0.003, 0.03, 0.004, 0.12),
         (0.0012, 0.0015, 0.00062, 0.07, 2.9, 1.9, 0.0036, 0.05, 0.012, 0.06)]
ORDER = {}


def R(b, lo, hi, st=1):
    b, off = PIECES.get(b, (b, 0))
    return (b, lo + off, hi + off, st)


def build(T, rank, n_ranks, topo, core):
    ops = []

    def ap(r):
        if len(r) == 2:
            return ap(r[0]).indirect(ap(r[1]))
        b, lo, hi, st = r
        if st < 0:
            return T[b][:, hi - 1:(lo - 1 if lo > 0 else None):st]
        return T[b][:, lo:hi] if st == 1 else T[b][:, lo:hi:st]

    def flat(rs):
        out = []
        for r in rs:
            if isinstance(r, tuple):
                out += list(r) if len(r) == 2 else [r]
        return out

    def n_of(r):
        return 16 * n_of(r[1]) if len(r) == 2 else len(range(r[1], r[2], abs(r[3])))

    def two(rs):
        return all(SCRATCH[r[0]][2] in ("bfloat16", "uint16") for r in rs)

    def sc(s):
        return ap(s) if isinstance(s, tuple) else s

    def add(q, fn, rd, wr, t, kind="c"):
        ops.append([q, fn, flat(rd), flat(wr), t, kind])

    def vt(o, i, k, fix=0.05):
        return (fix, n_of(i), 1) if len(i) == 2 else (fix - 0.05, max(64, n_of(o) * k), 0, 1, 7)

    def tt(o, a, b, op):
        k = 1 if len(a) == 2 or "psum" in (SCRATCH[a[0]][0], SCRATCH[b[0]][0]) else 2
        add("v", lambda g: g.vector.tensor_tensor(ap(o), ap(a), ap(b), op), [a, b], [o], vt(o, a, k))

    def ts(o, a, s1, s2, op0, op1=None):
        k = 0.5 if len(a) == 4 and two([o, a]) else 1
        if op1 is None:
            add("v", lambda g: g.vector.tensor_scalar(ap(o), ap(a), sc(s1), None, op0), [a, s1], [o], vt(o, a, k))
        else:
            add("v", lambda g: g.vector.tensor_scalar(ap(o), ap(a), sc(s1), sc(s2), op0, op1), [a, s1, s2], [o], vt(o, a, k))

    def cp(o, a):
        add("v", lambda g: g.vector.tensor_copy(ap(o), ap(a)), [a], [o], vt(o, a, 1))

    def ms(o, c):
        c = int(c) if SCRATCH[o[0]][2] == "int32" else float(c)
        add("v", lambda g: g.vector.memset(ap(o), c), [], [o], vt(o, o, 0.5 if two([o]) else 1))

    def scan(o, a, b, init, op0, op1):
        add("v", lambda g: g.vector.tensor_tensor_scan(ap(o), ap(a), ap(b), init, op0, op1), [a, b], [o],
            vt(o, a, 0.5 if two([o, a, b]) else 1))

    def act(o, a, f, **kw):
        add("s", lambda g: g.scalar.activation(ap(o), ap(a), f, **kw), [a], [o], vt(o, a, 1, 0.085))

    def copy(q, o, a):
        if q == "s":
            act(o, a, F.Copy)
        else:
            cp(o, a)

    def mms(items, start=True, stop=True):
        for k, run in enumerate(items):
            def fn(g, run=run, first=start and k == 0, end=stop and k == len(items) - 1):
                for m, (o, l, r) in enumerate(run):
                    ins = g.tensor.matmul(ap(o), ap(l), ap(r), first and m == 0, end and m == len(run) - 1)
                return ins
            add("t", fn, [x for o, l, r in run for x in (l, r)], [o for o, l, r in run],
                (0.0, sum(max(64, n_of(r)) * (1 if two([r]) else 4) for o, l, r in run), 2, len(run), 8, 1, 7))

    def total(o, terms, start=True, stop=True):
        mms([[(o, l, r) for l, r in terms]], start, stop)

    def iota(o, pat, base, ch=0):
        kw = {} if SCRATCH[o[0]][2] == "int32" else {"allow_small_or_imprecise_dtypes": True}
        add("g", lambda g: g.iota(ap(o), pat, base, ch, **kw), [], [o], (0.0, 160 + 2 * n_of(o), 0))

    def fill(o, c):
        iota(o, [[0, n_of(o)]], int(c))

    def dma(q, o, a, rd, wr, kib):
        add(q, (lambda g: g.sync.dma_start(o, a)) if q == "y" else (lambda g: g.scalar.dma_start(o, a)), rd, wr,
            (1.2, kib, 6), "dma")

    def swap(buf, n, up, down, sem, first):
        sends = ([(T.cores[rank - 1], up)] if rank > 0 else []) + ([(T.cores[rank + 1], down)] if rank < n_ranks - 1 else [])
        sends.sort(key=lambda s: len(topo.engines(core, s[0])))
        used, trs = [], []
        for to, (so, do) in sends:
            en = [x for x in topo.engines(core, to) if x not in used][:NE]
            used += en
            rid, pid, _ = topo.addr(to)
            trs.append(RemoteDMATransfer(dst_ids=[DstId(rid=rid, pnc=pid)], dma_engine_mask=sum(1 << x for x in en),
                                         remote_sem=T.sem[sem], src=T[buf][:, so:so + n], dst=T[buf][:, do:do + n]))
        wr = ([R(buf, down[1], down[1] + n)] if rank > 0 else []) + ([R(buf, up[1], up[1] + n)] if rank < n_ranks - 1 else [])
        add("g", lambda g: g.remote_dma_fused(trs, local_sem=T.sem.ls), [R(buf, up[0], up[0] + n), R(buf, down[0], down[0] + n)],
            wr, (0.0, 1, 10 if first else 4), ("rem", sem, len(used)))

    bank = [0]

    def pb(n):
        bank[0] = (bank[0] + 1) % 3
        return R("pb%d" % bank[0], 0, n)

    def L(b, lo=0):
        return R(b, lo, lo + 128)

    def wide(b, c0, c1, off=0):
        return R(b, off + 16 * c0, off + 16 * c1)

    def py(h):
        return R("py%d" % (h // 64), 0, 64)

    def px(h):
        return R("ps" if h else "pz", 128, 192)

    P, PZ, PF = R("col", 0, 1), R("col", 3, 4), R("col", 4, 5)
    Ew = R("E", 0, 8192)
    Id, nId, kId, hId, I37, I101, Fd, nFd = (L(x) for x in ("Id", "nId", "kId", "hId", "I37", "I101", "Fd", "nFd"))
    zw = L("zf", 8)
    edges, twice = R("sl", 0, 1), R("sl", 2, 3)

    def Z(c0, c1, st=1):
        return R("zf", 8 + c0, 8 + c1, st)

    for d in range(DAYS):
        if rank == 0:
            ms(R("MB%d" % d, 128, 224), 512)
        if rank == n_ranks - 1:
            ms(R("MB%d" % d, 0, 96), -512)
    extra = len(ops)
    dma("y", T.Bt[:, :], T.boat[:, :], [], [L("Bt")], 64)
    dma("y", T.X[:, :], T.x[:, :], [], [R("X", 0, 2048)], 576)
    dma("y", T.E[:, :], T.enc[:, :], [], [Ew], 2624)

    def thresholds(name, segs, less, put):
        put(L(name), 21 - less)
        for c0, c1, rt in segs:
            if rt == "S":
                put(R(name, c0, c1), 10 - less)
        ms(R(name, 0, 128, 32), 128)

    iota(R("ik", 0, 1), [[0, 1]], 0, 1)
    iota(L("i1"), [[16, 4], [64, 32]], 0)
    iota(R("i4", 0, 8), [[1, 4], [64, 2]], 0)
    iota(L("iI"), [[1, 128]], 0, -1)
    iota(R("iq", 0, 144), [[1, 144]], -15)
    iota(L("i2"), [[1, 128]], 0)
    iota(L("i5"), [[0, 4], [8192, 32]], 811)
    iota(L("cols"), [[1, 128]], 0)
    iota(L("i6"), [[0, 8], [1, 16]], 0)
    iota(R("rw", 0, 8), [[-31, 2], [32, 4]], 31)
    iota(R("rw", 8, 16), [[-29, 2], [32, 4]], 30)
    iota(R("rw", 16, 32), [[1, 4], [32, 4]], 0)
    iota(R("rw", 32, 48), [[4, 2], [0, 2], [1, 4]], 0)
    iota(R("i4", 8, 16), [[4, 8]], 0)
    thresholds("b0", SEG0, 0, fill)
    fill(R("ka", 0, 96), 0)
    for d in range(DAYS):
        k = 811 * (4 - d)
        if d < DAYS - 1:
            fill(R("T%d" % (d + 1), 0, ZN), 0)
            fill(R("ka", 32 * d, 32 * d + 8), k - k % 64)
            fill(R("ka", 32 * d + 16, 32 * d + 24), k % 64)
        fill(R("MB%d" % d, 96, 128), 0)
        if d == 0:
            fill(R("bs", 0, 16), 21)
            fill(L("zt"), 0)
    thresholds("b2", SEG_LAST, 64, fill)
    iota(L("i3"), [[16, 8], [0, 16]], 0)
    thresholds("bF", SEG_FIRST, 0, ms)
    thresholds("b1", SEG1, 64, ms)
    for r, c in ((R("T0", 0, ZN), 0), (R("B", 0, 1), 0), (R("neg", 0, 64), -1), (R("val", 128, 129), 0), (R("bb", 128, 129), 0),
                 (R("rv", 0, 1), -65536), (R("tau", 128, 129), BIG), (R("Lc", 0, 1), 0), (R("pv", 0, 1), 0),
                 (R("s", 64, 137, 72), 0), (R("m", 0, 16), 0)):
        ms(r, c)
    ts(R("ik", 1, 2), R("ik", 0, 1), 15, None, A.bitwise_and)
    ts(R("ik", 2, 3), R("ik", 0, 1), 112, None, A.bitwise_and)
    cp(R("col", 0, 2), R("ik", 1, 3))
    ts(R("col", 2, 3), P, 4.0, None, A.mult)
    ts(PZ, P, float(ZN), None, A.add)
    ts(PF, P, float(FAR), None, A.add)
    ts(R("sP", 0, 8), R("i4", 0, 8), R("col", 2, 3), None, A.add)
    ts(L("op"), L("i1"), P, None, A.add)
    for mat, w in ((Id, 1.0), (nId, -1.0), (hId, BIG / 2), (kId, -32 * BIG), (I37, 37.0), (I101, 101.0), (Fd, 1.0), (nFd, -1.0)):
        ts(mat, L("iI"), 0.0, w, A.is_equal, A.mult)
    ts(R("W", 0, 144), R("iq", 0, 144), R("col", 1, 2), -BIG, A.is_equal, A.mult)
    ts(L("BO"), L("i3"), R("col", 1, 2), None, A.is_equal)
    ts(L("pv", 128), L("i2"), 65536.0, None, A.mult)
    cp(L("pv", 256), L("i5"))
    ts(L("keep"), L("i6"), P, None, A.is_equal)
    tt(R("rm", 0, 48), R("rw", 0, 48), R("keep", 0, 48), A.mult)
    ts(L("thr"), L("keep"), -64.0, 74.5, A.mult, A.add)
    ts(L("keep"), L("i6"), 0.0, None, A.not_equal)
    scan(R("rw", 0, 48), R("keep", 0, 48), R("rm", 0, 48), 0.0, A.mult, A.add)
    cp(R("sl", 0, 3), R("rw", 15, 48, 16))
    ts(R("sQ", 0, 8), R("i4", 8, 16), R("rw", 31, 32), None, A.add)

    def opening(h, name, left=None):
        total(py(h), [(hId, R(name, h, h + 64))] + ([(kId, R(left, h, h + 64))] if left else []), True, False)

    def reduce(y, cb, c0, c1, stop=True):
        total(y, [(R("W", 15 - p, 143 - p), R(cb, 16 * c0 + p, 16 * c1, 16)) for p in range(16)], False, stop)

    def columns(o, mine, rival, a, b, c0, c1):
        if isinstance(rival, tuple):
            tt(R(a, c0, c1), mine, rival, A.add)
        else:
            ts(R(a, c0, c1), mine, rival, None, A.add)
        ts(R(b, c0, c1), R(a, c0, c1), 8191, None, A.bitwise_and)
        cp(R(o, c0, c1), R(b, c0, c1))

    def morning(t, c0, c1):
        ts(R("PA", c0, c1), Z(c0, c1), 37.0, 37 * HALF + 811 * t + LIFT, A.mult, A.add)
        ts(R("B", c0 + 1, c1 + 1), Z(c0, c1), 101.0, 101 * HALF, A.mult, A.add)
        columns("oc0", R("PA", c0, c1), R("B", c0, c1), "ci", "cj", c0, c1)

    def values(patched):
        ts(L("Bm"), L("B", 1), 8191, None, A.bitwise_and)
        tt(L("vB"), L("Bm"), L("pv", 256), A.add)
        tt(L("val"), Z(0, 128), L("pv", 128), A.add)
        if patched:
            act(R("vB", 0, 128, 32), Z(0, 128, 32), F.Identity, scale=101.0, bias=101 * HALF + 811.0 - LIFT)

    def halves(done, stop=True):
        if done in (64, 128):
            reduce(py(done - 64), "C", done - 64, done, stop)

    def race(rt, c0, c1, eg, xs, xq):
        q = pb(16 * (c1 - c0))
        if rt == "S":
            act(wide("G1", c0, c1), eg, F.Copy)
            mms([[(q, nId, xq), (q, Id, xs)], [(q, Id, wide("G1", c0, c1))]])
            act(wide("C", c0, c1), q, F.Sign, bias=-0.5)
        else:
            total(q, [(Id, xq), (nId, xs)])
            act(wide("D", c0, c1), q, F.Copy)
            tt(wide("C", c0, c1), eg, wide("D", c0, c1), A.is_gt)

    ts(zw, (L("Bt"), R("sP", 0, 8)), -HALF, None, A.add)
    morning(0, 0, 128)
    values(False)
    for h in (0, 64):
        opening(h, "bF")
    for c0 in range(0, 128, 32):
        act(wide("T0", c0, c0 + 32, ZN), (R("X", 0, 2048), R("op", c0, c0 + 32)), F.Copy)
        q = pb(512)
        total(q, [(Id, wide("T0", c0 - 1, c0 + 31, ZN)), (nId, wide("T0", c0, c0 + 32, ZN))])
        act(wide("D", c0, c0 + 32), q, F.Copy)
    for c0, c1, rt in SEG_FIRST:
        eg = (Ew, R("oc0", c0, c1))
        if rt == "V":
            tt(wide("C", c0, c1), eg, wide("D", c0, c1), A.is_gt)
        else:
            act(wide("G1", c0, c1), eg, F.Copy)
            q = pb(16 * (c1 - c0))
            mms([[(q, nId, wide("D", c0, c1))], [(q, Id, wide("G1", c0, c1))]])
            act(wide("C", c0, c1), q, F.Sign, bias=-0.5)
        halves(c1)

    for d in range(DAYS):
        Tn, Tx, MB, last = "T%d" % d, "T%d" % (d + 1), "MB%d" % d, d == DAYS - 1
        Tw = R(Tn, 0, TW)
        for h in (0, 64):
            scan(R("tau", h, h + 64), R("neg", 0, 64), py(h), 1.0, A.mult, A.max)
        tt(L("n"), L("tau"), L("tau", 1), A.min)
        scan(L("Lc", 1), L("n"), L("cols"), 0.0, A.max, A.min)
        ts(L("orv"), L("Lc"), 16.0, PZ, A.mult, A.add)
        scan(R("pv", 1, 128), R("n", 0, 127), R("vB", 0, 127), 0.0, A.max, A.min)
        columns("oc1", L("PA"), L("pv"), "ci", "cj", 0, 128)
        act(L("sgn"), L("n"), F.Sign, scale=-1.0)
        act(L("nr"), L("sgn"), F.Relu)
        for h in (0, 64):
            opening(h, "b2" if last else "b1", "sgn")
        scan(L("rv", 1), L("n"), L("val"), -65536.0, A.max, A.min)
        tt(L("pv", 384), L("rv", 1), L("rv"), A.subtract)
        scan(L("bb"), L("tau"), L("val"), 0.0, A.max, A.min)
        for h in (0, 64):
            total(px(h), [(Fd, R("bb", h, h + 64)), (nFd, R("bb", h + 1, h + 65)), (Fd, R("val", h + 1, h + 65))], True, False)
        for c0, c1, rt in SEG_LAST if last else SEG1:
            eg, xr, xs = (Ew, R("oc1", c0, c1)), (Tw, R("orv", c0, c1)), wide(Tn, c0, c1, ZN)
            if rt == "V":
                tt(wide("D", c0, c1), eg, xs, A.add)
                tt(wide("C", c0, c1), xr, wide("D", c0, c1), A.is_lt)
            else:
                act(wide("G2", c0, c1), xr, F.Copy)
                race(rt, c0, c1, eg, xs, wide("G2", c0, c1))
            halves(c1)
        for h in (0, 64):
            def H(b, sh=0, st=1):
                return R(b, h + sh, h + 64 + sh, st)
            pad = h // 8
            scan(H("u"), py(h), H("sgn"), 0.0, A.max, A.mult)
            tt(H("e"), H("u"), H("pv", 384), A.min)
            scan(H("s", pad, -1), H("nr", 0, -1), H("e", 0, -1), 0.0, A.mult, A.max)
            total(px(h), [(nFd, H("s", pad)), (Fd, H("s", pad + 1))], False, True)
            ts(H("hi"), px(h), TO65536, TO65536, A.add, A.subtract)
            if not last:
                ts(H("op"), H("hi"), 2.0 ** -12, PZ, A.mult, A.add)
            tt(Z(h, h + 64), px(h), H("hi"), A.subtract)
            if not last:
                opening(h, "b0")
                morning(2 * d + 2, h, h + 64)
        nb = 8 if last else 16

        def M(lo, n=4):
            return R(MB, lo, lo + n)

        def S(lo, n=4):
            return R("ps", lo, lo + n)
        ts(R("oE", 0, 16), (L("hi"), edges), 2.0 ** -12, PZ, A.mult, A.add)
        cp(M(288, 16), (zw, edges))
        tt(M(304, 16), (zw, edges), M(288, 16), A.subtract)
        act(M(224, 64), (Tw, R("oE", 0, 4)), F.Copy)
        act(M(320, 64), (Tw, R("oE", 4, 8)), F.Copy)
        swap(MB, 96, (288, 0), (224, 128), "ar%d" % d, d == 0)
        own = [(S(4 * k), (I101, I37)[k % 2], M(288 + 16 * j + 4 * k)) for k in range(nb // 4) for j in range(2)]
        far = [(S(4 * k), (I37, I101)[k % 2], M((4, 192)[k % 2] + 16 * j)) for k in range(nb // 4) for j in range(2)]
        mms([[(S(0, nb), Id, R("ka", 32 * d, 32 * d + nb))] + own], True, False)
        if last:
            ts(L("op"), (L("hi"), R("sQ", 0, 8)), 2.0 ** -12, PZ, A.mult, A.add)
            for c0, c1, q in FIN:
                copy(q, wide("XO", c0, c1), (Tw, R("op", c0, c1)))
                dma("y", T.yx[:, 16 * c0:16 * c1], T.XO[:, 16 * c0:16 * c1], [wide("XO", c0, c1)], [], 256)
            ts(L("ZO"), (zw, R("sQ", 0, 8)), HALF, None, A.add)
        else:
            act(M(384, 128), (Tw, R("oE", 8, 16)), F.Copy)
            values(True)
            for c0, c1, rt in SEG0:
                xs = wide(Tx, c0, c1, ZN)
                copy("v" if rt == "X" else "s", xs, (Tw, R("op", c0, c1)))
                race(rt, c0, c1, (Ew, R("oc0", c0, c1)), xs, wide(Tx, c0 - 1, c1 - 1, ZN))
                halves(c1, False)
        mms([far + [(S(0, nb), Id, R("ka", 32 * d + 16, 32 * d + 16 + nb))]], False, True)
        columns("om", S(0, nb), 138 * HALF + 811 * (2 * DAYS + d if last else 2 * d + 2), "sm", "sn", 0, nb)
        q = pb(16 * nb)
        for k, (ahead, behind) in enumerate(((224, 32), (128, 320), (384, 32), (128, 448))[:nb // 4]):
            total(R(q[0], 64 * k, 64 * k + 64), [(Id, M(ahead, 64)), (nId, M(behind, 64))])
        act(wide("Ds", 0, nb), q, F.Copy)
        tt(wide("Cs", 0, nb), (Ew, R("om", 0, nb)), wide("Ds", 0, nb), A.is_gt)
        gap = R(q[0], 256, 264)
        mms([[(gap, Id, M(288, 8))] + [(R(q[0], 256 + 4 * k, 260 + 4 * k), nId, M((4, 192)[k] + 16 * j))
                                       for k in range(2) for j in range(2)] + [(gap, Id, M(304, 8))]])
        if last:
            cnt = pb(128)
            total(cnt, [(L("BO"), wide("Cs", 0, 8))])
            ts(L("mw"), cnt, 10.5, None, A.is_gt)
            tt(L("u"), cnt, L("thr"), A.is_gt)
            tt(L("pv"), L("mw"), q, A.mult)
            tt(R("XE", 0, 64), M(224, 64), R("pv", 0, 64), A.subtract)
            tt(R("XE", 64, 128), M(320, 64), R("pv", 64, 128), A.add)
            dma("s", T.yx[:, 0:64], T.XE[:, 64:128], [R("XE", 64, 128)], [], 16)
            dma("y", T.yx[:, 1984:2048], T.XE[:, 0:64], [R("XE", 0, 64)], [], 16)
            scan(L("n"), L("keep"), L("u"), 0.0, A.mult, A.add)
            tt(R("dz", 0, 8), gap, R("n", 15, 128, 16), A.mult)
            tt(R("ZO", 124, 128), R("ZO", 124, 128), R("dz", 0, 4), A.subtract)
            tt(R("ZO", 0, 4), R("ZO", 0, 4), R("dz", 4, 8), A.subtract)
            dma("y", T.yb[:, :], T.ZO[:, :], [L("ZO")], [], 64)
            break
        for k, w in enumerate((37.0, 1.0, 101.0, 1.0)):
            act(R("gap", 4 * k, 4 * k + 4), R(q[0], 256 + 4 * (k // 2), 260 + 4 * (k // 2)), F.Copy, scale=w)
        total(S(16, 16), [(hId, R("bs", 0, 16))], True, False)
        reduce(S(16, 16), "Cs", 0, 16)
        ts(R("m", 0, 8), S(16, 8), 0.0, -1.0, A.is_lt, A.mult)
        tt(R("zt", 31, 128, 32), S(24), R("m", 0, 4), A.mult)
        tt(R("zt", 1, 128, 32), S(28), R("m", 4, 8), A.mult)
        for h in (0, 64):
            total(py(h), [(kId, R("zt", h, h + 64))], False, True)
        tt(R("dz", 0, 16), (R("m", 0, 16), twice), R("gap", 0, 16), A.mult)
        tt(R("lv", 31, 415, 32), R("lv", 31, 415, 32), R("dz", 0, 12), A.add)
        tt(R("val", 0, 128, 32), R("val", 0, 128, 32), R("dz", 12, 16), A.add)
        ts(R("of", 0, 16, 2), R("m", 0, 8), float(FAR), PF, A.mult, A.add)
        for k in range(8):
            lo, c = (32, 128)[k // 4] + 16 * (k % 4), 32 * (k % 4) + (31, 0)[k // 4]
            act(wide(Tx, c, c + 1, ZN), (M(lo, FAR + 16), R("of", 2 * k, 2 * k + 1)), F.Copy)
    return ops, extra


def meets(a, b):
    if a[2] <= b[1] or b[2] <= a[1]:
        return False
    sa, sb = abs(a[3]), abs(b[3])
    return not (sa == sb and sa > 1 and (a[1] - b[1]) % sa)


def depend(ops):
    deps, hist = [], {}
    for i, (q, _, rd, wr, _, _) in enumerate(ops):
        dp = set()
        acc = [(r, False) for r in rd] + [(r, True) for r in wr]
        for r, w in acc:
            psum = SCRATCH[r[0]][0] == "psum"
            for j, r2, w2 in hist.get(r[0], []):
                if ((w or w2) and meets(r, r2)) or (psum and (ops[j][0] != q or q == "t")):
                    dp.add(j)
        for r, w in acc:
            hist.setdefault(r[0], []).append((i, r, w))
        deps.append(dp)
    anc = []
    for i, dp in enumerate(deps):
        far = 0
        for j in dp:
            far |= anc[j]
        deps[i] = sorted(j for j in dp if not far >> j & 1)
        for j in dp:
            far |= 1 << j
        anc.append(far if ops[i][5] in ("c", "dma") else 0)
    return deps


def times(ops, gs):
    gs = list(gs) + [gs[4] + gs[5]]
    return [o[4][0] + sum(n * gs[k] for n, k in zip(o[4][1::2], o[4][2::2])) for o in ops]


def lag(ops, i, j, gs):
    return gs[3] if ops[j][0] != "t" else 0.0 if ops[i][0] == "t" else gs[3] + gs[9]


def span(ops, deps, seq, gs):
    t, free, end = times(ops, gs), {}, {}
    for i in seq:
        q = ops[i][0]
        st = max([free.get(q, 0.0)] + [end[j] + lag(ops, i, j, gs) for j in deps[i]])
        end[i] = st + t[i]
        free[q] = end[i] if ops[i][5] == "c" else st + 0.1
    return max(end.values())


def place(ops, edges, hold, keys):
    start, busy = [0.0] * len(ops), {q: [] for q in "vstgy"}
    for i in keys:
        st = max([0.0] + [start[j] + x for j, x in edges[i]])
        b, h = busy[ops[i][0]], hold[i]
        k = len(b)
        while k and b[k - 1][0] >= st:
            k -= 1
        if k and b[k - 1][1] > st:
            st = b[k - 1][1]
        while k < len(b) and b[k][0] < st + h - 1e-9:
            st = b[k][1]
            k += 1
        b.insert(k, (st, st + h))
        start[i] = st
    return start


def search(ops, deps):
    rng = np.random.default_rng(SEED)
    n, gs = len(ops), GUESS[0]
    t = times(ops, gs)
    hold = [t[i] if ops[i][5] == "c" else 0.1 for i in range(n)]
    fw, prev = [], {}
    for i in range(n):
        e = [(j, t[j] + lag(ops, i, j, gs)) for j in deps[i]]
        if ops[i][0] in "yg":
            if ops[i][0] in prev:
                e.append((prev[ops[i][0]], hold[prev[ops[i][0]]]))
            prev[ops[i][0]] = i
        fw.append(e)
    bw = [[] for _ in range(n)]
    for i in range(n):
        for j, x in fw[i]:
            bw[j].append((i, x - hold[j] + hold[i]))
    known = [(times(ops, x), [[(j, lag(ops, i, j, x)) for j in deps[i]] for i in range(n)]) for x in GUESS]

    def spans(seq):
        out = 0.0
        for tx, ex in known:
            free, end = {}, [0.0] * n
            for i in seq:
                q = ops[i][0]
                st = max([free.get(q, 0.0)] + [end[j] + x for j, x in ex[i]])
                end[i] = st + tx[i]
                free[q] = end[i] if ops[i][5] == "c" else st + 0.1
            out += max(end)
        return out

    def legal(key):
        key = list(key)
        for i in range(n):
            key[i] = max([key[i]] + [key[j] + 1e-6 for j, _ in fw[i]])
        return sorted(range(n), key=lambda i: (key[i], i))

    def sweep(key):
        st = place(ops, fw, hold, legal(key))
        end = max(st[i] + t[i] for i in range(n))
        e2 = [bw[i] + ([] if bw[i] else [(n, t[i] - hold[i])]) for i in range(n)]
        back = place(ops + [ops[0]], e2 + [[]], hold + [0.0], [n] + legal([st[i] + hold[i] for i in range(n)])[::-1])
        st = place(ops, fw, hold, legal([end - back[i] - hold[i] for i in range(n)]))
        seq = legal(st)
        return spans(seq), st, seq

    def shake(state, tries):
        for _ in range(tries):
            key = list(state[1])
            mid, wid, amp = rng.random() * max(key), 1.0 + 6.0 * rng.random(), 1.5 * rng.random()
            new = sweep([x + float(rng.normal()) * amp if abs(x - mid) < wid else x for x in key])
            if new[0] <= state[0]:
                state = new
        return state

    first = sweep([float(i) for i in range(n)])
    low, _, seq = shake(min(shake(first, TRIES // (2 * STARTS)) for _ in range(STARTS)), TRIES // 2)
    for _ in range(MOVES):
        at = {x: k for k, x in enumerate(seq)}
        k = int(rng.integers(n))
        i = seq[k]
        lo = max([k - 12, 0] + [at[j] + 1 for j, _ in fw[i]])
        hi = min([k + 12, n - 1] + [at[j] - 1 for j, _ in bw[i]])
        to = int(rng.integers(lo, hi + 1))
        if any(ops[x][0] == ops[i][0] for x in seq[min(k, to):max(k, to) + 1] if x != i):
            new = seq[:k] + seq[k + 1:]
            new.insert(to, i)
            c = spans(new)
            if c <= low:
                low, seq = c, new
    ORDER["low"] = low
    return seq


def rank_program(g, core, T, topo):
    rank = T.rank_of(core)
    if rank is None:
        return
    n_ranks = len(T.cores)
    if "seq" not in ORDER:
        mid = build(T, 1, n_ranks, topo, T.cores[1])[0]
        ORDER["seq"] = search(mid, depend(mid))
    ops, extra = build(T, rank, n_ranks, topo, core)
    deps = depend(ops)
    seq = list(range(extra)) + [i + extra for i in ORDER["seq"]]
    pos, cnt, at = {}, {}, {}
    for k, i in enumerate(seq):
        ch = ops[i][0] if ops[i][5] == "c" else i
        cnt[ch] = cnt.get(ch, 0) + 1
        pos[i], at[i] = (ch, cnt[ch]), k
    known = {q: {} for q in "vstgy"}
    clock, waits, marked = {}, {}, set()
    for i in seq:
        q = ops[i][0]
        kn, ws = known[q], []
        for j in sorted(deps[i], key=lambda j: -at[j]):
            ch, p = pos[j]
            if not (q == "t" and ch == "t") and kn.get(ch, 0) < p:
                ws.append(j)
                marked.add(j)
                for c2, p2 in clock[j].items():
                    kn[c2] = max(kn.get(c2, 0), p2)
        waits[i] = ws
        clock[i] = dict(kn) if ops[i][5] in ("c", "dma") else {}
        clock[i][pos[i][0]] = pos[i][1]
    eng = {"v": g.vector, "s": g.scalar, "t": g.tensor, "g": g, "y": g.sync}
    count, sem, nd, sent, tail = {}, {}, 0, 0, []
    for i in seq:
        q, fn, _, wr, _, kind = ops[i]
        for j in waits[i]:
            eng[q].wait_ge(*sem[j])
        ins = fn(g)
        if kind == "dma":
            sem[i] = (T.sem["dm%d" % nd], 16)
            nd += 1
            ins.then_inc(*sem[i])
            if i not in marked:
                tail.append((q, sem[i]))
        elif kind == "c":
            if i in marked:
                count[q] = count.get(q, 0) + 1
                sem[i] = (T.sem["q" + q], count[q])
                ins.then_inc(sem[i][0], 1)
        else:
            sem[i] = (T.sem[kind[1]], NE * len(wr))
            sent += kind[2]
    for q, s in tail:
        eng[q].wait_ge(*s)
    g.wait_ge(T.sem.ls, sent)
